import numpy as np
import ml_dtypes


def mxq(x, axis, fmt="e4m3"):
    dtype, down = {"e4m3": (ml_dtypes.float8_e4m3fn, 7), "e5m2": (ml_dtypes.float8_e5m2, 14)}[fmt]
    v = np.moveaxis(np.asarray(x, np.float32).astype(ml_dtypes.bfloat16).astype(np.float64), axis, -1)
    blocks = v.reshape(v.shape[:-1] + (-1, 32))
    amax = np.abs(blocks).max(-1, keepdims=True)
    byte = np.maximum(np.where(amax > 0, np.frexp(amax)[1] - 1 + 127, 0) - down, 1)
    scale = np.exp2(byte - 127.0)
    codes = (blocks / scale).astype(np.float32).astype(dtype).astype(np.float64)
    return np.moveaxis((codes * scale).reshape(v.shape), -1, axis)


WIDE = False


def mx_kscale(k):
    if not WIDE:
        return np.ones(k)
    levels = np.array([10, -10, 5, -5, 0])
    if k % 512:
        return np.exp2(np.random.permutation(np.resize(levels, k // 32))).repeat(32)
    a = np.empty((k // 512, 16))
    for p in range(k // 512):
        a[p, :8] = np.random.permutation(np.resize(levels, 8))
        for g in range(8):
            far = levels[np.abs(levels - a[p, g]) >= 10]
            a[p, g + 8] = far[np.random.randint(len(far))]
    return np.exp2(a.ravel()).repeat(32)


def f64(x):
    return np.asarray(x).astype(np.float64)


def striped(idx):
    return np.tile(np.asarray(idx).reshape(-1, 16).T, (8, 1)).astype(np.uint16)


def unstriped(offs):
    return offs[:16].T.reshape(-1).astype(np.int64)


E2M1 = np.array([0.0, 0.5, 1.0, 1.5, 2.0, 3.0, 4.0, 6.0, -0.0, -0.5, -1.0, -1.5, -2.0, -3.0, -4.0, -6.0])


def pack_weight(w, fmt):
    k, n = w.shape
    w = f64(np.asarray(w, np.float32).astype(ml_dtypes.bfloat16)).reshape(k // 32, 32, n)
    amax = np.abs(w).max(1)
    if fmt == "e4m3":
        byte = np.frexp(amax)[1] - 1 + 127 - 7
    else:
        mant, ex = np.frexp(amax / 6.0)
        byte = np.where(mant > 0.5, ex, ex - 1) + 127
    byte = np.clip(np.where(amax > 0, byte, 1), 1, 254)
    scaled = (w * np.exp2(127.0 - byte)[:, None, :]).reshape(k, n).astype(np.float32)
    by_word = np.ascontiguousarray(scaled.reshape(k // 512, 128, 4, n).transpose(0, 1, 3, 2))
    if fmt == "e4m3":
        words = by_word.astype(ml_dtypes.float8_e4m3fn).view(np.uint8)
    else:
        c = by_word.astype(ml_dtypes.float4_e2m1fn).view(np.uint8) & 0xF
        words = (c[..., 0::2] | (c[..., 1::2] << 4)).reshape(k // 512, 128, 2 * n)
    return np.ascontiguousarray(words), np.ascontiguousarray(byte.astype(np.uint8).reshape(k // 512, 16, n))


def unpack_weight(words, scales, fmt):
    g, _, n = scales.shape
    words = np.ascontiguousarray(words).reshape(g, 128, n, -1)
    if fmt == "e4m3":
        vals = words.view(ml_dtypes.float8_e4m3fn).astype(np.float64)
    else:
        nib = np.empty((g, 128, n, 4), np.uint8)
        nib[..., 0::2] = words & 0xF
        nib[..., 1::2] = words >> 4
        vals = E2M1[nib]
    vals = vals * np.repeat(np.exp2(scales.astype(np.float64) - 127.0), 8, axis=1)[..., None]
    return vals.transpose(0, 1, 3, 2).reshape(g * 512, n)


def rot(x):
    y = x.reshape(-1, 2, x.shape[1])
    return np.stack([-y[:, 1], y[:, 0]], axis=1).reshape(x.shape)


K, T, I, D, U = 512, 2048, 512, 512, 1024


def setup_inputs():
    n = np.random.standard_normal
    idx = np.random.permutation(T)[:I]
    idx2 = np.random.randint(0, U, I)
    fk = mx_kscale(K)
    embp = pack_weight(n((K, T)) / fk[:, None], "e2m1")
    return {
        "emb_words": embp[0],
        "emb_scales": embp[1],
        "wk": (n((K, D)) * 1 / np.sqrt(K) * fk[:, None]).astype(np.float32),
        "cosn": (np.repeat(np.round(np.cos(np.arange(D // 2)[:, None] * 0.11 + np.arange(U)[None] * 0.37) * 64) / 64, 2, axis=0)).astype(np.float32),
        "sinn": (np.repeat(np.round(np.sin(np.arange(D // 2)[:, None] * 0.11 + np.arange(U)[None] * 0.37) * 64) / 64, 2, axis=0)).astype(np.float32),
        "offs": striped(idx),
        "offs2": striped(idx2),
    }


def reference(emb_words, emb_scales, wk, cosn, sinn, offs, offs2):
    idx = unstriped(offs)
    idx2 = unstriped(offs2)
    embu = unpack_weight(emb_words, emb_scales, "e2m1")
    wkq = mxq(f64(wk), 0, "e4m3")
    embidxg = embu[:, idx]
    b = wkq.T @ embidxg
    br = rot(b)
    y = b * f64(cosn)[:, idx2] + br * f64(sinn)[:, idx2]
    return y

@@ -1,0 +1,129 @@
+from contextlib import ExitStack
+
+import concourse.mybir as mybir
+
+K, T, I, D, U = 512, 2048, 512, 512, 1024
+FLOPS = 2 * K * D * I
+BYTES = 128 * 4096 + 16 * 2048 + K * D * 4 + 2 * (D // 2) * U * 4 + 2 * 128 * 32 * 2 + D * I * 4
+
+F32 = mybir.dt.float32
+BF16 = mybir.dt.bfloat16
+I32 = mybir.dt.int32
+U32 = mybir.dt.uint32
+U16 = mybir.dt.uint16
+U8 = mybir.dt.uint8
+FP8X4 = mybir.dt.float8_e4m3fn_x4
+FP4X4 = mybir.dt.float4_e2m1fn_x4
+MULT = mybir.AluOpType.mult
+ADD = mybir.AluOpType.add
+SUB = mybir.AluOpType.subtract
+
+P = 128
+PACK = 4
+HALVES = 2
+HALF = D // HALVES
+
+
+def tile_attend_freshrope_kernel(tc, emb_words, emb_scales, wk, cosn, sinn, offs, offs2, out):
+    nc = tc.nc
+    with ExitStack() as ctx:
+        keep = ctx.enter_context(tc.tile_pool(name="keep", bufs=1))
+        psum = ctx.enter_context(tc.psum_pool(name="psum", bufs=1))
+
+        tok_list = keep.tile([P, I // 16], U16, name="tok_list")
+        pos_list = keep.tile([P, I // 16], U16, name="pos_list")
+        words = keep.tile([P, T], U16, name="words", align_bytes=64)
+        scales = keep.tile([P, T], U8, name="scales", align_bytes=64)
+        cos_all = [keep.tile([P, U], F32, name="cos_all%d" % h) for h in range(HALVES)]
+        sin_all = [keep.tile([P, U], F32, name="sin_all%d" % h) for h in range(HALVES)]
+        w_raw = [keep.tile([P, PACK, HALF], F32, name="w_raw%d" % h) for h in range(HALVES)]
+
+        cos_rows = cosn.rearrange("(h p e) u -> h e p u", h=HALVES, e=2)
+        sin_rows = sinn.rearrange("(h p e) u -> h e p u", h=HALVES, e=2)
+        w_rows = wk.rearrange("(p j) (h c) -> h p j c", j=PACK, h=HALVES)
+        out_rows = out.rearrange("(h p e) i -> h e p i", h=HALVES, e=2)
+
+        nc.vector.memset(scales[:].bitcast(I32), 0)
+        nc.sync.dma_start(tok_list[:], offs)
+        nc.sync.dma_start(words[:].bitcast(I32), emb_words[0].bitcast(I32))
+        nc.sync.dma_start(pos_list[:], offs2)
+        for q in range(4):
+            nc.sync.dma_start(
+                scales[32 * q : 32 * q + 4, :].bitcast(I32),
+                emb_scales[0, 4 * q : 4 * q + 4, :].bitcast(I32),
+            )
+        nc.sync.dma_start(w_raw[0][:], w_rows[0])
+        nc.sync.dma_start(cos_all[0][:], cos_rows[0, 0])
+        nc.sync.dma_start(sin_all[0][:], sin_rows[0, 0])
+        nc.sync.dma_start(w_raw[1][:], w_rows[1])
+        nc.sync.dma_start(cos_all[1][:], cos_rows[1, 0])
+        nc.sync.dma_start(sin_all[1][:], sin_rows[1, 0])
+
+        emb_w = keep.tile([P, I], U16, name="emb_w", align_bytes=64)
+        emb_s = keep.tile([P, I], U8, name="emb_s", align_bytes=64)
+        cos_g = [keep.tile([P, I], F32, name="cos_g%d" % h) for h in range(HALVES)]
+        sin_g = [keep.tile([P, I], F32, name="sin_g%d" % h) for h in range(HALVES)]
+        w_bf = [keep.tile([P, 2, P * PACK], BF16, name="w_bf%d" % h, align_bytes=64) for h in range(HALVES)]
+        w_codes = [keep.tile([P, HALF], U32, name="w_codes%d" % h, align_bytes=64) for h in range(HALVES)]
+        w_scales = [keep.tile([P, HALF], U8, name="w_scales%d" % h, align_bytes=64) for h in range(HALVES)]
+        acc = [[psum.tile([P, I], F32, name="acc%d%d" % (h, e)) for e in range(2)] for h in range(HALVES)]
+        by_cos = [[keep.tile([P, I], F32, name="by_cos%d%d" % (h, e)) for e in range(2)] for h in range(HALVES)]
+        by_sin = [[keep.tile([P, I], F32, name="by_sin%d%d" % (h, e)) for e in range(2)] for h in range(HALVES)]
+        keys = [[keep.tile([P, I], F32, name="keys%d%d" % (h, e)) for e in range(2)] for h in range(HALVES)]
+        staged = [keep.tile([P, I], F32, name="staged%d" % e) for e in range(2)]
+
+        def deal(copy, h, e):
+            copy(
+                w_bf[h][:, e, :].rearrange("p (m j) -> p m j", j=PACK),
+                w_raw[h][:].rearrange("p j (m e) -> p e m j", e=2)[:, e],
+            )
+
+        def project(h, e):
+            cols = slice(e * P, (e + 1) * P)
+            nc.vector.quantize_mx(
+                out=w_codes[h][:, cols].bitcast(FP8X4),
+                scales=w_scales[h][:, cols],
+                in_=w_bf[h][:, e, :],
+            )
+            nc.tensor.matmul_mx(
+                out=acc[h][e][:],
+                lhsT=w_codes[h][:, cols].bitcast(FP8X4),
+                lhsT_scale=w_scales[h][:, cols],
+                rhs=emb_w[:].bitcast(FP4X4),
+                rhs_scale=emb_s[:],
+                start=True,
+                stop=True,
+            )
+
+        def finish(adder, h, e, slots):
+            adder.tensor_tensor(keys[h][e][:, slots], by_cos[h][e][:, slots], by_sin[h][e][:, slots], ADD if e else SUB)
+            nc.sync.dma_start(out_rows[h, e][:, slots], keys[h][e][:, slots])
+
+        every = slice(0, I)
+        nc.vector.tensor_copy(emb_w[:], words[:].indirect(tok_list[:]))
+        nc.vector.tensor_copy(emb_s[:], scales[:].indirect(tok_list[:]))
+        deal(nc.scalar.copy, 0, 0)
+        deal(nc.scalar.copy, 0, 1)
+        project(0, 0)
+        nc.vector.tensor_copy(cos_g[0][:], cos_all[0][:].indirect(pos_list[:]))
+        project(0, 1)
+        nc.vector.tensor_copy(sin_g[0][:], sin_all[0][:].indirect(pos_list[:]))
+        for e in range(2):
+            nc.scalar.copy(staged[e][:], acc[0][e][:])
+            nc.gpsimd.tensor_tensor(by_cos[0][e][:], staged[e][:], cos_g[0][:], MULT)
+        for e in range(2):
+            nc.vector.tensor_tensor(by_sin[0][e][:], acc[0][1 - e][:], sin_g[0][:], MULT)
+        for e in range(2):
+            finish(nc.gpsimd, 0, e, every)
+        for e in range(2):
+            deal(nc.scalar.copy, 1, e)
+        project(1, 0)
+        nc.vector.tensor_copy(cos_g[1][:], cos_all[1][:].indirect(pos_list[:]))
+        project(1, 1)
+        nc.vector.tensor_copy(sin_g[1][:], sin_all[1][:].indirect(pos_list[:]))
+        for e in range(2):
+            for s in range(2):
+                slots = slice(s * I // 2, (s + 1) * I // 2)
+                nc.vector.tensor_tensor(by_cos[1][e][:, slots], acc[1][e][:, slots], cos_g[1][:, slots], MULT)
+                nc.vector.tensor_tensor(by_sin[1][e][:, slots], acc[1][1 - e][:, slots], sin_g[1][:, slots], MULT)
+                finish(nc.vector if e == 1 and s == 1 else nc.gpsimd, 1, e, slots)

@@ -70,7 +70,6 @@ def tile_attend_freshrope_kernel(tc, emb_words, emb_scales, wk, cosn, sinn, offs
         by_cos = [[keep.tile([P, I], F32, name="by_cos%d%d" % (h, e)) for e in range(2)] for h in range(HALVES)]
         by_sin = [[keep.tile([P, I], F32, name="by_sin%d%d" % (h, e)) for e in range(2)] for h in range(HALVES)]
         keys = [[keep.tile([P, I], F32, name="keys%d%d" % (h, e)) for e in range(2)] for h in range(HALVES)]
-        staged = [keep.tile([P, I], F32, name="staged%d" % e) for e in range(2)]
 
         def deal(copy, h, e):
             copy(
@@ -109,12 +108,9 @@ def tile_attend_freshrope_kernel(tc, emb_words, emb_scales, wk, cosn, sinn, offs
         project(0, 1)
         nc.vector.tensor_copy(sin_g[0][:], sin_all[0][:].indirect(pos_list[:]))
         for e in range(2):
-            nc.scalar.copy(staged[e][:], acc[0][e][:])
-            nc.gpsimd.tensor_tensor(by_cos[0][e][:], staged[e][:], cos_g[0][:], MULT)
-        for e in range(2):
+            nc.vector.tensor_tensor(by_cos[0][e][:], acc[0][e][:], cos_g[0][:], MULT)
             nc.vector.tensor_tensor(by_sin[0][e][:], acc[0][1 - e][:], sin_g[0][:], MULT)
-        for e in range(2):
-            finish(nc.gpsimd, 0, e, every)
+            finish(nc.vector if e else nc.gpsimd, 0, e, every)
         for e in range(2):
             deal(nc.scalar.copy, 1, e)
         project(1, 0)

@@ -22,6 +22,7 @@ P = 128
 PACK = 4
 HALVES = 2
 HALF = D // HALVES
+EARLY = 128
 
 
 def tile_attend_freshrope_kernel(tc, emb_words, emb_scales, wk, cosn, sinn, offs, offs2, out):
@@ -35,7 +36,7 @@ def tile_attend_freshrope_kernel(tc, emb_words, emb_scales, wk, cosn, sinn, offs
         words = keep.tile([P, T], U16, name="words", align_bytes=64)
         scales = keep.tile([P, T], U8, name="scales", align_bytes=64)
         cos_all = [keep.tile([P, U], F32, name="cos_all%d" % h) for h in range(HALVES)]
-        sin_all = [keep.tile([P, U], F32, name="sin_all%d" % h) for h in range(HALVES)]
+        sin_all = [keep.tile([P, U], F32, name="sin_all%d" % h, tag="sin_all%d" % h) for h in range(HALVES)]
         w_raw = [keep.tile([P, PACK, HALF], F32, name="w_raw%d" % h) for h in range(HALVES)]
 
         cos_rows = cosn.rearrange("(h p e) u -> h e p u", h=HALVES, e=2)
@@ -44,14 +45,11 @@ def tile_attend_freshrope_kernel(tc, emb_words, emb_scales, wk, cosn, sinn, offs
         out_rows = out.rearrange("(h p e) i -> h e p i", h=HALVES, e=2)
 
         nc.vector.memset(scales[:].bitcast(I32), 0)
-        nc.sync.dma_start(tok_list[:], offs)
         nc.sync.dma_start(words[:].bitcast(I32), emb_words[0].bitcast(I32))
+        nc.sync.dma_start(tok_list[:], offs)
         nc.sync.dma_start(pos_list[:], offs2)
-        for q in range(4):
-            nc.sync.dma_start(
-                scales[32 * q : 32 * q + 4, :].bitcast(I32),
-                emb_scales[0, 4 * q : 4 * q + 4, :].bitcast(I32),
-            )
+        for r in range(4):
+            nc.sync.dma_start(scales[r:P:32, :].bitcast(I32), emb_scales[0, r:16:4, :].bitcast(I32))
         nc.sync.dma_start(w_raw[0][:], w_rows[0])
         nc.sync.dma_start(cos_all[0][:], cos_rows[0, 0])
         nc.sync.dma_start(sin_all[0][:], sin_rows[0, 0])
@@ -69,7 +67,6 @@ def tile_attend_freshrope_kernel(tc, emb_words, emb_scales, wk, cosn, sinn, offs
         acc = [[psum.tile([P, I], F32, name="acc%d%d" % (h, e)) for e in range(2)] for h in range(HALVES)]
         by_cos = [[keep.tile([P, I], F32, name="by_cos%d%d" % (h, e)) for e in range(2)] for h in range(HALVES)]
         by_sin = [[keep.tile([P, I], F32, name="by_sin%d%d" % (h, e)) for e in range(2)] for h in range(HALVES)]
-        keys = [[keep.tile([P, I], F32, name="keys%d%d" % (h, e)) for e in range(2)] for h in range(HALVES)]
 
         def deal(copy, h, e):
             copy(
@@ -94,11 +91,15 @@ def tile_attend_freshrope_kernel(tc, emb_words, emb_scales, wk, cosn, sinn, offs
                 stop=True,
             )
 
-        def finish(adder, h, e, slots):
-            adder.tensor_tensor(keys[h][e][:, slots], by_cos[h][e][:, slots], by_sin[h][e][:, slots], ADD if e else SUB)
-            nc.sync.dma_start(out_rows[h, e][:, slots], keys[h][e][:, slots])
+        def multiply(h, e, slots):
+            nc.vector.tensor_tensor(by_cos[h][e][:, slots], acc[h][e][:, slots], cos_g[h][:, slots], MULT)
+            nc.vector.tensor_tensor(by_sin[h][e][:, slots], acc[h][1 - e][:, slots], sin_g[h][:, slots], MULT)
 
-        every = slice(0, I)
+        def finish(adder, h, e, slots, tag):
+            keys = keep.tile([P, slots.stop - slots.start], F32, name="keys%d%d%d" % (h, e, slots.start), tag=tag)
+            adder.tensor_tensor(keys[:], by_cos[h][e][:, slots], by_sin[h][e][:, slots], ADD if e else SUB)
+            nc.sync.dma_start(out_rows[h, e][:, slots], keys[:])
+
         nc.vector.tensor_copy(emb_w[:], words[:].indirect(tok_list[:]))
         nc.vector.tensor_copy(emb_s[:], scales[:].indirect(tok_list[:]))
         deal(nc.scalar.copy, 0, 0)
@@ -107,19 +108,23 @@ def tile_attend_freshrope_kernel(tc, emb_words, emb_scales, wk, cosn, sinn, offs
         nc.vector.tensor_copy(cos_g[0][:], cos_all[0][:].indirect(pos_list[:]))
         project(0, 1)
         nc.vector.tensor_copy(sin_g[0][:], sin_all[0][:].indirect(pos_list[:]))
-        for e in range(2):
-            nc.vector.tensor_tensor(by_cos[0][e][:], acc[0][e][:], cos_g[0][:], MULT)
-            nc.vector.tensor_tensor(by_sin[0][e][:], acc[0][1 - e][:], sin_g[0][:], MULT)
-            finish(nc.vector if e else nc.gpsimd, 0, e, every)
+        low, high = slice(0, I // 2), slice(I // 2, I)
+        early, late = slice(0, EARLY), slice(EARLY, I)
+        for e, slots in ((0, low), (0, high), (1, early)):
+            multiply(0, e, slots)
+            finish(nc.gpsimd, 0, e, slots, "keys0%d%d" % (e, slots.start))
+        multiply(0, 1, late)
         for e in range(2):
             deal(nc.scalar.copy, 1, e)
         project(1, 0)
         nc.vector.tensor_copy(cos_g[1][:], cos_all[1][:].indirect(pos_list[:]))
         project(1, 1)
         nc.vector.tensor_copy(sin_g[1][:], sin_all[1][:].indirect(pos_list[:]))
-        for e in range(2):
-            for s in range(2):
-                slots = slice(s * I // 2, (s + 1) * I // 2)
-                nc.vector.tensor_tensor(by_cos[1][e][:, slots], acc[1][e][:, slots], cos_g[1][:, slots], MULT)
-                nc.vector.tensor_tensor(by_sin[1][e][:, slots], acc[1][1 - e][:, slots], sin_g[1][:, slots], MULT)
-                finish(nc.vector if e == 1 and s == 1 else nc.gpsimd, 1, e, slots)
+        finish(nc.gpsimd, 0, 1, late, "sin_all1")
+        for slots in (low, high):
+            multiply(1, 0, slots)
+            finish(nc.gpsimd, 1, 0, slots, "keys10%d" % slots.start)
+        for slots in (low, high):
+            multiply(1, 1, slots)
+        for slots in (low, high):
+            finish(nc.vector, 1, 1, slots, "keys11%d" % slots.start)

@@ -1,6 +1,7 @@
 from contextlib import ExitStack
 
 import concourse.mybir as mybir
+from concourse.masks import make_identity
 
 K, T, I, D, U = 512, 2048, 512, 512, 1024
 FLOPS = 2 * K * D * I
@@ -22,7 +23,6 @@ P = 128
 PACK = 4
 HALVES = 2
 HALF = D // HALVES
-EARLY = 128
 
 
 def tile_attend_freshrope_kernel(tc, emb_words, emb_scales, wk, cosn, sinn, offs, offs2, out):
@@ -36,7 +36,7 @@ def tile_attend_freshrope_kernel(tc, emb_words, emb_scales, wk, cosn, sinn, offs
         words = keep.tile([P, T], U16, name="words", align_bytes=64)
         scales = keep.tile([P, T], U8, name="scales", align_bytes=64)
         cos_all = [keep.tile([P, U], F32, name="cos_all%d" % h) for h in range(HALVES)]
-        sin_all = [keep.tile([P, U], F32, name="sin_all%d" % h, tag="sin_all%d" % h) for h in range(HALVES)]
+        sin_all = [keep.tile([P, U], F32, name="sin_all%d" % h, tag="sin_all%d" % h, align_bytes=64) for h in range(HALVES)]
         w_raw = [keep.tile([P, PACK, HALF], F32, name="w_raw%d" % h) for h in range(HALVES)]
 
         cos_rows = cosn.rearrange("(h p e) u -> h e p u", h=HALVES, e=2)
@@ -45,8 +45,8 @@ def tile_attend_freshrope_kernel(tc, emb_words, emb_scales, wk, cosn, sinn, offs
         out_rows = out.rearrange("(h p e) i -> h e p i", h=HALVES, e=2)
 
         nc.vector.memset(scales[:].bitcast(I32), 0)
-        nc.sync.dma_start(words[:].bitcast(I32), emb_words[0].bitcast(I32))
         nc.sync.dma_start(tok_list[:], offs)
+        nc.sync.dma_start(words[:].bitcast(I32), emb_words[0].bitcast(I32))
         nc.sync.dma_start(pos_list[:], offs2)
         for r in range(4):
             nc.sync.dma_start(scales[r:P:32, :].bitcast(I32), emb_scales[0, r:16:4, :].bitcast(I32))
@@ -59,72 +59,96 @@ def tile_attend_freshrope_kernel(tc, emb_words, emb_scales, wk, cosn, sinn, offs
 
         emb_w = keep.tile([P, I], U16, name="emb_w", align_bytes=64)
         emb_s = keep.tile([P, I], U8, name="emb_s", align_bytes=64)
-        cos_g = [keep.tile([P, I], F32, name="cos_g%d" % h) for h in range(HALVES)]
-        sin_g = [keep.tile([P, I], F32, name="sin_g%d" % h) for h in range(HALVES)]
-        w_bf = [keep.tile([P, 2, P * PACK], BF16, name="w_bf%d" % h, align_bytes=64) for h in range(HALVES)]
         w_codes = [keep.tile([P, HALF], U32, name="w_codes%d" % h, align_bytes=64) for h in range(HALVES)]
         w_scales = [keep.tile([P, HALF], U8, name="w_scales%d" % h, align_bytes=64) for h in range(HALVES)]
         acc = [[psum.tile([P, I], F32, name="acc%d%d" % (h, e)) for e in range(2)] for h in range(HALVES)]
         by_cos = [[keep.tile([P, I], F32, name="by_cos%d%d" % (h, e)) for e in range(2)] for h in range(HALVES)]
         by_sin = [[keep.tile([P, I], F32, name="by_sin%d%d" % (h, e)) for e in range(2)] for h in range(HALVES)]
 
-        def deal(copy, h, e):
-            copy(
-                w_bf[h][:, e, :].rearrange("p (m j) -> p m j", j=PACK),
-                w_raw[h][:].rearrange("p j (m e) -> p e m j", e=2)[:, e],
-            )
+        def deal(h, tag):
+            w_bf = keep.tile([P, 2, P * PACK], BF16, name="w_bf%d" % h, tag=tag, align_bytes=64)
+            for e in range(2):
+                nc.scalar.copy(
+                    w_bf[:, e, :].rearrange("p (m j) -> p m j", j=PACK),
+                    w_raw[h][:].rearrange("p j (m e) -> p e m j", e=2)[:, e],
+                )
+            return w_bf
 
-        def project(h, e):
-            cols = slice(e * P, (e + 1) * P)
+        def project(h, w_bf):
             nc.vector.quantize_mx(
-                out=w_codes[h][:, cols].bitcast(FP8X4),
-                scales=w_scales[h][:, cols],
-                in_=w_bf[h][:, e, :],
+                out=w_codes[h][:].bitcast(FP8X4),
+                scales=w_scales[h][:],
+                in_=w_bf[:].rearrange("p e c -> p (e c)"),
             )
-            nc.tensor.matmul_mx(
-                out=acc[h][e][:],
-                lhsT=w_codes[h][:, cols].bitcast(FP8X4),
-                lhsT_scale=w_scales[h][:, cols],
-                rhs=emb_w[:].bitcast(FP4X4),
-                rhs_scale=emb_s[:],
-                start=True,
-                stop=True,
-            )
+            for e in range(2):
+                cols = slice(e * P, (e + 1) * P)
+                nc.tensor.matmul_mx(
+                    out=acc[h][e][:],
+                    lhsT=w_codes[h][:, cols].bitcast(FP8X4),
+                    lhsT_scale=w_scales[h][:, cols],
+                    rhs=emb_w[:].bitcast(FP4X4),
+                    rhs_scale=emb_s[:],
+                    start=True,
+                    stop=True,
+                )
 
-        def multiply(h, e, slots):
-            nc.vector.tensor_tensor(by_cos[h][e][:, slots], acc[h][e][:, slots], cos_g[h][:, slots], MULT)
-            nc.vector.tensor_tensor(by_sin[h][e][:, slots], acc[h][1 - e][:, slots], sin_g[h][:, slots], MULT)
+        def look_up(table, tag):
+            picked = keep.tile([P, I], F32, name="picked", tag=tag, align_bytes=64)
+            nc.vector.tensor_copy(picked[:], table[:].indirect(pos_list[:]))
+            return picked
 
-        def finish(adder, h, e, slots, tag):
-            keys = keep.tile([P, slots.stop - slots.start], F32, name="keys%d%d%d" % (h, e, slots.start), tag=tag)
+        def multiply(h, e, slots, cos_g, sin_g):
+            for bank in range(2):
+                product, factor = (by_cos, cos_g) if bank == e else (by_sin, sin_g)
+                nc.vector.tensor_tensor(product[h][e][:, slots], acc[h][bank][:, slots], factor[:, slots], MULT)
+
+        def finish(adder, h, e, slots):
+            keys = keep.tile([P, slots.stop - slots.start], F32, name="keys%d%d%d" % (h, e, slots.start))
             adder.tensor_tensor(keys[:], by_cos[h][e][:, slots], by_sin[h][e][:, slots], ADD if e else SUB)
             nc.sync.dma_start(out_rows[h, e][:, slots], keys[:])
 
+        def finish_on_tensor(h, e):
+            turned_sum = psum.tile([P, I], F32, name="turned_sum")
+            turned = keep.tile([P, I], F32, name="turned")
+            upright = psum.tile([P, I], F32, name="upright")
+            keys = keep.tile([P, I], F32, name="keys_tensor")
+            blocks = [slice(t * P, (t + 1) * P) for t in range(I // P)]
+            turns = [(product, b) for product in (by_sin, by_cos) for b in blocks]
+            for n, (product, b) in enumerate(turns):
+                nc.tensor.matmul(
+                    turned_sum[:, b],
+                    product[h][e][:, b],
+                    identity[:],
+                    start=n == 0,
+                    stop=n == len(turns) - 1,
+                    is_transpose=True,
+                )
+            nc.scalar.copy(turned[:], turned_sum[:])
+            for b in blocks:
+                nc.tensor.transpose(upright[:, b], turned[:, b], identity[:])
+            nc.scalar.copy(keys[:], upright[:])
+            nc.sync.dma_start(out_rows[h, e], keys[:])
+
+        identity = keep.tile([P, P], F32, name="identity")
+        make_identity(nc, identity[:])
         nc.vector.tensor_copy(emb_w[:], words[:].indirect(tok_list[:]))
         nc.vector.tensor_copy(emb_s[:], scales[:].indirect(tok_list[:]))
-        deal(nc.scalar.copy, 0, 0)
-        deal(nc.scalar.copy, 0, 1)
-        project(0, 0)
-        nc.vector.tensor_copy(cos_g[0][:], cos_all[0][:].indirect(pos_list[:]))
-        project(0, 1)
-        nc.vector.tensor_copy(sin_g[0][:], sin_all[0][:].indirect(pos_list[:]))
-        low, high = slice(0, I // 2), slice(I // 2, I)
-        early, late = slice(0, EARLY), slice(EARLY, I)
-        for e, slots in ((0, low), (0, high), (1, early)):
-            multiply(0, e, slots)
-            finish(nc.gpsimd, 0, e, slots, "keys0%d%d" % (e, slots.start))
-        multiply(0, 1, late)
-        for e in range(2):
-            deal(nc.scalar.copy, 1, e)
-        project(1, 0)
-        nc.vector.tensor_copy(cos_g[1][:], cos_all[1][:].indirect(pos_list[:]))
-        project(1, 1)
-        nc.vector.tensor_copy(sin_g[1][:], sin_all[1][:].indirect(pos_list[:]))
-        finish(nc.gpsimd, 0, 1, late, "sin_all1")
+        every, low, high = slice(0, I), slice(0, I // 2), slice(I // 2, I)
+        w_bf = deal(0, "sin_g")
+        cos_g = look_up(cos_all[0], "cos_g")
+        project(0, w_bf)
+        sin_g = look_up(sin_all[0], "sin_g")
+        multiply(0, 0, every, cos_g, sin_g)
+        finish(nc.gpsimd, 0, 0, every)
+        multiply(0, 1, every, cos_g, sin_g)
+        finish_on_tensor(0, 1)
+        project(1, deal(1, "sin_all0"))
+        cos_g = look_up(cos_all[1], "cos_g")
+        sin_g = look_up(sin_all[1], "sin_g")
         for slots in (low, high):
-            multiply(1, 0, slots)
-            finish(nc.gpsimd, 1, 0, slots, "keys10%d" % slots.start)
+            multiply(1, 0, slots, cos_g, sin_g)
+            finish(nc.gpsimd, 1, 0, slots)
         for slots in (low, high):
-            multiply(1, 1, slots)
+            multiply(1, 1, slots, cos_g, sin_g)
         for slots in (low, high):
-            finish(nc.vector, 1, 1, slots, "keys11%d" % slots.start)
+            finish(nc.vector, 1, 1, slots)

@@ -127,7 +127,7 @@ def tile_attend_freshrope_kernel(tc, emb_words, emb_scales, wk, cosn, sinn, offs
             for b in blocks:
                 nc.tensor.transpose(upright[:, b], turned[:, b], identity[:])
             nc.scalar.copy(keys[:], upright[:])
-            nc.sync.dma_start(out_rows[h, e], keys[:])
+            nc.scalar.dma_start(out_rows[h, e], keys[:])
 
         identity = keep.tile([P, P], F32, name="identity")
         make_identity(nc, identity[:])
@@ -138,8 +138,9 @@ def tile_attend_freshrope_kernel(tc, emb_words, emb_scales, wk, cosn, sinn, offs
         cos_g = look_up(cos_all[0], "cos_g")
         project(0, w_bf)
         sin_g = look_up(sin_all[0], "sin_g")
-        multiply(0, 0, every, cos_g, sin_g)
-        finish(nc.gpsimd, 0, 0, every)
+        for slots in (low, high):
+            multiply(0, 0, slots, cos_g, sin_g)
+            finish(nc.gpsimd, 0, 0, slots)
         multiply(0, 1, every, cos_g, sin_g)
         finish_on_tensor(0, 1)
         project(1, deal(1, "sin_all0"))

@@ -1,7 +1,6 @@
 from contextlib import ExitStack
 
 import concourse.mybir as mybir
-from concourse.masks import make_identity
 
 K, T, I, D, U = 512, 2048, 512, 512, 1024
 FLOPS = 2 * K * D * I
@@ -18,11 +17,14 @@ FP4X4 = mybir.dt.float4_e2m1fn_x4
 MULT = mybir.AluOpType.mult
 ADD = mybir.AluOpType.add
 SUB = mybir.AluOpType.subtract
+COPY = mybir.ActivationFunctionType.Copy
 
 P = 128
 PACK = 4
 HALVES = 2
 HALF = D // HALVES
+RUNS = 2
+RUN = I // RUNS
 
 
 def tile_attend_freshrope_kernel(tc, emb_words, emb_scales, wk, cosn, sinn, offs, offs2, out):
@@ -36,120 +38,95 @@ def tile_attend_freshrope_kernel(tc, emb_words, emb_scales, wk, cosn, sinn, offs
         words = keep.tile([P, T], U16, name="words", align_bytes=64)
         scales = keep.tile([P, T], U8, name="scales", align_bytes=64)
         cos_all = [keep.tile([P, U], F32, name="cos_all%d" % h) for h in range(HALVES)]
-        sin_all = [keep.tile([P, U], F32, name="sin_all%d" % h, tag="sin_all%d" % h, align_bytes=64) for h in range(HALVES)]
+        sin_all = [keep.tile([P, U], F32, name="sin_all%d" % h) for h in range(HALVES)]
         w_raw = [keep.tile([P, PACK, HALF], F32, name="w_raw%d" % h) for h in range(HALVES)]
 
         cos_rows = cosn.rearrange("(h p e) u -> h e p u", h=HALVES, e=2)
         sin_rows = sinn.rearrange("(h p e) u -> h e p u", h=HALVES, e=2)
         w_rows = wk.rearrange("(p j) (h c) -> h p j c", j=PACK, h=HALVES)
-        out_rows = out.rearrange("(h p e) i -> h e p i", h=HALVES, e=2)
+        out_rows = out.rearrange("(h p e) i -> h p e i", h=HALVES, e=2)
 
         nc.vector.memset(scales[:].bitcast(I32), 0)
         nc.sync.dma_start(tok_list[:], offs)
-        nc.sync.dma_start(words[:].bitcast(I32), emb_words[0].bitcast(I32))
-        nc.sync.dma_start(pos_list[:], offs2)
         for r in range(4):
             nc.sync.dma_start(scales[r:P:32, :].bitcast(I32), emb_scales[0, r:16:4, :].bitcast(I32))
+        nc.sync.dma_start(words[:].bitcast(I32), emb_words[0].bitcast(I32))
         nc.sync.dma_start(w_raw[0][:], w_rows[0])
+        nc.sync.dma_start(pos_list[:], offs2)
         nc.sync.dma_start(cos_all[0][:], cos_rows[0, 0])
-        nc.sync.dma_start(sin_all[0][:], sin_rows[0, 0])
         nc.sync.dma_start(w_raw[1][:], w_rows[1])
+        nc.sync.dma_start(sin_all[0][:], sin_rows[0, 0])
         nc.sync.dma_start(cos_all[1][:], cos_rows[1, 0])
         nc.sync.dma_start(sin_all[1][:], sin_rows[1, 0])
 
         emb_w = keep.tile([P, I], U16, name="emb_w", align_bytes=64)
         emb_s = keep.tile([P, I], U8, name="emb_s", align_bytes=64)
+        w_bf = [keep.tile([P, 2, P * PACK], BF16, name="w_bf%d" % h, align_bytes=64) for h in range(HALVES)]
         w_codes = [keep.tile([P, HALF], U32, name="w_codes%d" % h, align_bytes=64) for h in range(HALVES)]
         w_scales = [keep.tile([P, HALF], U8, name="w_scales%d" % h, align_bytes=64) for h in range(HALVES)]
-        acc = [[psum.tile([P, I], F32, name="acc%d%d" % (h, e)) for e in range(2)] for h in range(HALVES)]
-        by_cos = [[keep.tile([P, I], F32, name="by_cos%d%d" % (h, e)) for e in range(2)] for h in range(HALVES)]
-        by_sin = [[keep.tile([P, I], F32, name="by_sin%d%d" % (h, e)) for e in range(2)] for h in range(HALVES)]
+        acc = [[psum.tile([P, 2, RUN], F32, name="acc%d%d" % (h, s)) for s in range(RUNS)] for h in range(HALVES)]
+        by_cos = [[keep.tile([P, 2, RUN], F32, name="by_cos%d%d" % (h, s)) for s in range(RUNS)] for h in range(HALVES)]
+        by_sin = [[keep.tile([P, 2, RUN], F32, name="by_sin%d%d" % (h, s)) for s in range(RUNS)] for h in range(HALVES)]
 
-        def deal(h, tag):
-            w_bf = keep.tile([P, 2, P * PACK], BF16, name="w_bf%d" % h, tag=tag, align_bytes=64)
-            for e in range(2):
-                nc.scalar.copy(
-                    w_bf[:, e, :].rearrange("p (m j) -> p m j", j=PACK),
-                    w_raw[h][:].rearrange("p j (m e) -> p e m j", e=2)[:, e],
-                )
-            return w_bf
+        def deal_on_vector(h):
+            nc.vector.tensor_copy(
+                w_bf[h][:].rearrange("p e (a b j) -> p a j b e", b=2, j=PACK),
+                w_raw[h][:].rearrange("p j (a b e) -> p a j b e", b=2, e=2),
+            )
 
-        def project(h, w_bf):
+        def project(h):
             nc.vector.quantize_mx(
                 out=w_codes[h][:].bitcast(FP8X4),
                 scales=w_scales[h][:],
-                in_=w_bf[:].rearrange("p e c -> p (e c)"),
+                in_=w_bf[h][:].rearrange("p e c -> p (e c)"),
             )
-            for e in range(2):
-                cols = slice(e * P, (e + 1) * P)
-                nc.tensor.matmul_mx(
-                    out=acc[h][e][:],
-                    lhsT=w_codes[h][:, cols].bitcast(FP8X4),
-                    lhsT_scale=w_scales[h][:, cols],
-                    rhs=emb_w[:].bitcast(FP4X4),
-                    rhs_scale=emb_s[:],
-                    start=True,
-                    stop=True,
-                )
+            for s in range(RUNS):
+                slots = slice(s * RUN, (s + 1) * RUN)
+                for e in range(2):
+                    cols = slice(e * P, (e + 1) * P)
+                    nc.tensor.matmul_mx(
+                        out=acc[h][s][:, e, :],
+                        lhsT=w_codes[h][:, cols].bitcast(FP8X4),
+                        lhsT_scale=w_scales[h][:, cols],
+                        rhs=emb_w[:, slots].bitcast(FP4X4),
+                        rhs_scale=emb_s[:, slots],
+                        start=True,
+                        stop=True,
+                    )
 
-        def look_up(table, tag):
-            picked = keep.tile([P, I], F32, name="picked", tag=tag, align_bytes=64)
-            nc.vector.tensor_copy(picked[:], table[:].indirect(pos_list[:]))
+        def look_up(table, name, s):
+            picked = keep.tile([P, RUN], F32, name=name)
+            nc.scalar.activation(picked[:], table[:].indirect(pos_list[:, s * RUN // 16 : (s + 1) * RUN // 16]), COPY)
             return picked
 
-        def multiply(h, e, slots, cos_g, sin_g):
-            for bank in range(2):
-                product, factor = (by_cos, cos_g) if bank == e else (by_sin, sin_g)
-                nc.vector.tensor_tensor(product[h][e][:, slots], acc[h][bank][:, slots], factor[:, slots], MULT)
+        def times_cos(h, s):
+            picked = look_up(cos_all[h], "cos_g%d%d" % (h, s), s)
+            nc.vector.tensor_tensor(by_cos[h][s][:], acc[h][s][:], picked[:].unsqueeze(1).to_broadcast([P, 2, RUN]), MULT)
 
-        def finish(adder, h, e, slots):
-            keys = keep.tile([P, slots.stop - slots.start], F32, name="keys%d%d%d" % (h, e, slots.start))
-            adder.tensor_tensor(keys[:], by_cos[h][e][:, slots], by_sin[h][e][:, slots], ADD if e else SUB)
-            nc.sync.dma_start(out_rows[h, e][:, slots], keys[:])
+        def times_sin(h, s):
+            picked = look_up(sin_all[h], "sin_g%d%d" % (h, s), s)
+            nc.vector.scalar_tensor_tensor(by_sin[h][s][:, 0, :], acc[h][s][:, 1, :], -1.0, picked[:], MULT, MULT)
+            nc.vector.tensor_tensor(by_sin[h][s][:, 1, :], acc[h][s][:, 0, :], picked[:], MULT)
 
-        def finish_on_tensor(h, e):
-            turned_sum = psum.tile([P, I], F32, name="turned_sum")
-            turned = keep.tile([P, I], F32, name="turned")
-            upright = psum.tile([P, I], F32, name="upright")
-            keys = keep.tile([P, I], F32, name="keys_tensor")
-            blocks = [slice(t * P, (t + 1) * P) for t in range(I // P)]
-            turns = [(product, b) for product in (by_sin, by_cos) for b in blocks]
-            for n, (product, b) in enumerate(turns):
-                nc.tensor.matmul(
-                    turned_sum[:, b],
-                    product[h][e][:, b],
-                    identity[:],
-                    start=n == 0,
-                    stop=n == len(turns) - 1,
-                    is_transpose=True,
-                )
-            nc.scalar.copy(turned[:], turned_sum[:])
-            for b in blocks:
-                nc.tensor.transpose(upright[:, b], turned[:, b], identity[:])
-            nc.scalar.copy(keys[:], upright[:])
-            nc.scalar.dma_start(out_rows[h, e], keys[:])
+        def finish(adder, h, s):
+            keys = keep.tile([P, 2, RUN], F32, name="keys%d%d" % (h, s))
+            adder.tensor_tensor(keys[:], by_cos[h][s][:], by_sin[h][s][:], ADD)
+            nc.sync.dma_start(out_rows[h][:, :, s * RUN : (s + 1) * RUN], keys[:])
 
-        identity = keep.tile([P, P], F32, name="identity")
-        make_identity(nc, identity[:])
-        nc.vector.tensor_copy(emb_w[:], words[:].indirect(tok_list[:]))
         nc.vector.tensor_copy(emb_s[:], scales[:].indirect(tok_list[:]))
-        every, low, high = slice(0, I), slice(0, I // 2), slice(I // 2, I)
-        w_bf = deal(0, "sin_g")
-        cos_g = look_up(cos_all[0], "cos_g")
-        project(0, w_bf)
-        sin_g = look_up(sin_all[0], "sin_g")
-        for slots in (low, high):
-            multiply(0, 0, slots, cos_g, sin_g)
-            finish(nc.gpsimd, 0, 0, slots)
-        multiply(0, 1, every, cos_g, sin_g)
-        finish_on_tensor(0, 1)
-        project(1, deal(1, "sin_all0"))
-        cos_g = look_up(cos_all[1], "cos_g")
-        sin_g = look_up(sin_all[1], "sin_g")
-        for slots in (low, high):
-            multiply(1, 0, slots, cos_g, sin_g)
-            finish(nc.gpsimd, 1, 0, slots)
-        for slots in (low, high):
-            multiply(1, 1, slots, cos_g, sin_g)
-        for slots in (low, high):
-            finish(nc.vector, 1, 1, slots)
+        nc.vector.tensor_copy(emb_w[:], words[:].indirect(tok_list[:]))
+        deal_on_vector(0)
+        project(0)
+        for s in range(RUNS):
+            times_cos(0, s)
+        deal_on_vector(1)
+        project(1)
+        for s in range(RUNS):
+            times_sin(0, s)
+            finish(nc.gpsimd, 0, s)
+        for s in range(RUNS):
+            times_cos(1, s)
+        for s in range(RUNS):
+            times_sin(1, s)
+        for s in range(RUNS):
+            finish(nc.vector, 1, s)

@@ -25,6 +25,7 @@ HALVES = 2
 HALF = D // HALVES
 RUNS = 2
 RUN = I // RUNS
+LAST_RUN = RUN // 2
 
 
 def tile_attend_freshrope_kernel(tc, emb_words, emb_scales, wk, cosn, sinn, offs, offs2, out):
@@ -39,94 +40,107 @@ def tile_attend_freshrope_kernel(tc, emb_words, emb_scales, wk, cosn, sinn, offs
         scales = keep.tile([P, T], U8, name="scales", align_bytes=64)
         cos_all = [keep.tile([P, U], F32, name="cos_all%d" % h) for h in range(HALVES)]
         sin_all = [keep.tile([P, U], F32, name="sin_all%d" % h) for h in range(HALVES)]
-        w_raw = [keep.tile([P, PACK, HALF], F32, name="w_raw%d" % h) for h in range(HALVES)]
+        w_raw = keep.tile([P, PACK, D], F32, name="w_raw")
 
         cos_rows = cosn.rearrange("(h p e) u -> h e p u", h=HALVES, e=2)
         sin_rows = sinn.rearrange("(h p e) u -> h e p u", h=HALVES, e=2)
-        w_rows = wk.rearrange("(p j) (h c) -> h p j c", j=PACK, h=HALVES)
         out_rows = out.rearrange("(h p e) i -> h p e i", h=HALVES, e=2)
 
         nc.vector.memset(scales[:].bitcast(I32), 0)
         nc.sync.dma_start(tok_list[:], offs)
+        nc.sync.dma_start(pos_list[:], offs2)
         for r in range(4):
             nc.sync.dma_start(scales[r:P:32, :].bitcast(I32), emb_scales[0, r:16:4, :].bitcast(I32))
+        nc.sync.dma_start(w_raw[:], wk.rearrange("(p j) c -> p j c", j=PACK))
         nc.sync.dma_start(words[:].bitcast(I32), emb_words[0].bitcast(I32))
-        nc.sync.dma_start(w_raw[0][:], w_rows[0])
-        nc.sync.dma_start(pos_list[:], offs2)
-        nc.sync.dma_start(cos_all[0][:], cos_rows[0, 0])
-        nc.sync.dma_start(w_raw[1][:], w_rows[1])
-        nc.sync.dma_start(sin_all[0][:], sin_rows[0, 0])
-        nc.sync.dma_start(cos_all[1][:], cos_rows[1, 0])
-        nc.sync.dma_start(sin_all[1][:], sin_rows[1, 0])
+        for h in range(HALVES):
+            nc.sync.dma_start(cos_all[h][:], cos_rows[h, 0])
+            nc.sync.dma_start(sin_all[h][:], sin_rows[h, 0])
 
-        emb_w = keep.tile([P, I], U16, name="emb_w", align_bytes=64)
+        emb_w = [keep.tile([P, RUN], U16, name="emb_w%d" % s, align_bytes=64) for s in range(RUNS)]
         emb_s = keep.tile([P, I], U8, name="emb_s", align_bytes=64)
-        w_bf = [keep.tile([P, 2, P * PACK], BF16, name="w_bf%d" % h, align_bytes=64) for h in range(HALVES)]
+        w_bf = [keep.tile([P, 2, P * PACK], BF16, name="w_bf%d" % h, tag="w_bf%d" % h, align_bytes=64) for h in range(HALVES)]
         w_codes = [keep.tile([P, HALF], U32, name="w_codes%d" % h, align_bytes=64) for h in range(HALVES)]
         w_scales = [keep.tile([P, HALF], U8, name="w_scales%d" % h, align_bytes=64) for h in range(HALVES)]
         acc = [[psum.tile([P, 2, RUN], F32, name="acc%d%d" % (h, s)) for s in range(RUNS)] for h in range(HALVES)]
-        by_cos = [[keep.tile([P, 2, RUN], F32, name="by_cos%d%d" % (h, s)) for s in range(RUNS)] for h in range(HALVES)]
-        by_sin = [[keep.tile([P, 2, RUN], F32, name="by_sin%d%d" % (h, s)) for s in range(RUNS)] for h in range(HALVES)]
+
+        def deal_on_scalar(h):
+            for e in range(2):
+                nc.scalar.activation(
+                    w_bf[h][:, e, :].rearrange("p (m j) -> p m j", j=PACK),
+                    w_raw[:, :, h * HALF : (h + 1) * HALF].rearrange("p j (m e) -> p e m j", e=2)[:, e],
+                    COPY,
+                )
 
         def deal_on_vector(h):
             nc.vector.tensor_copy(
                 w_bf[h][:].rearrange("p e (a b j) -> p a j b e", b=2, j=PACK),
-                w_raw[h][:].rearrange("p j (a b e) -> p a j b e", b=2, e=2),
+                w_raw[:, :, h * HALF : (h + 1) * HALF].rearrange("p j (a b e) -> p a j b e", b=2, e=2),
             )
 
-        def project(h):
+        def quantise(h):
             nc.vector.quantize_mx(
                 out=w_codes[h][:].bitcast(FP8X4),
                 scales=w_scales[h][:],
                 in_=w_bf[h][:].rearrange("p e c -> p (e c)"),
             )
-            for s in range(RUNS):
-                slots = slice(s * RUN, (s + 1) * RUN)
-                for e in range(2):
-                    cols = slice(e * P, (e + 1) * P)
-                    nc.tensor.matmul_mx(
-                        out=acc[h][s][:, e, :],
-                        lhsT=w_codes[h][:, cols].bitcast(FP8X4),
-                        lhsT_scale=w_scales[h][:, cols],
-                        rhs=emb_w[:, slots].bitcast(FP4X4),
-                        rhs_scale=emb_s[:, slots],
-                        start=True,
-                        stop=True,
-                    )
 
-        def look_up(table, name, s):
-            picked = keep.tile([P, RUN], F32, name=name)
-            nc.scalar.activation(picked[:], table[:].indirect(pos_list[:, s * RUN // 16 : (s + 1) * RUN // 16]), COPY)
+        def project(h, s):
+            slots = slice(s * RUN, (s + 1) * RUN)
+            for e in range(2):
+                cols = slice(e * P, (e + 1) * P)
+                nc.tensor.matmul_mx(
+                    out=acc[h][s][:, e, :],
+                    lhsT=w_codes[h][:, cols].bitcast(FP8X4),
+                    lhsT_scale=w_scales[h][:, cols],
+                    rhs=emb_w[s][:].bitcast(FP4X4),
+                    rhs_scale=emb_s[:, slots],
+                    start=True,
+                    stop=True,
+                )
+
+        def look_up(table, name, first, count):
+            picked = keep.tile([P, count], F32, name=name)
+            nc.scalar.activation(picked[:], table[:].indirect(pos_list[:, first // 16 : (first + count) // 16]), COPY)
             return picked
 
-        def times_cos(h, s):
-            picked = look_up(cos_all[h], "cos_g%d%d" % (h, s), s)
-            nc.vector.tensor_tensor(by_cos[h][s][:], acc[h][s][:], picked[:].unsqueeze(1).to_broadcast([P, 2, RUN]), MULT)
+        def times_cos(h, s, tag):
+            picked = look_up(cos_all[h], "cos_g%d%d" % (h, s), s * RUN, RUN)
+            product = keep.tile([P, 2, RUN], F32, name="by_cos", tag=tag, align_bytes=64)
+            nc.vector.tensor_tensor(product[:], acc[h][s][:], picked[:].unsqueeze(1).to_broadcast([P, 2, RUN]), MULT)
+            return product
 
-        def times_sin(h, s):
-            picked = look_up(sin_all[h], "sin_g%d%d" % (h, s), s)
-            nc.vector.scalar_tensor_tensor(by_sin[h][s][:, 0, :], acc[h][s][:, 1, :], -1.0, picked[:], MULT, MULT)
-            nc.vector.tensor_tensor(by_sin[h][s][:, 1, :], acc[h][s][:, 0, :], picked[:], MULT)
+        def times_sin(h, first, count):
+            picked = look_up(sin_all[h], "sin_g%d_%d" % (h, first), first, count)
+            bank = acc[h][first // RUN][:, :, first % RUN : first % RUN + count]
+            product = keep.tile([P, 2, count], F32, name="by_sin%d_%d" % (h, first))
+            nc.vector.scalar_tensor_tensor(product[:, 0, :], bank[:, 1, :], -1.0, picked[:], MULT, MULT)
+            nc.vector.tensor_tensor(product[:, 1, :], bank[:, 0, :], picked[:], MULT)
+            return product
 
-        def finish(adder, h, s):
-            keys = keep.tile([P, 2, RUN], F32, name="keys%d%d" % (h, s))
-            adder.tensor_tensor(keys[:], by_cos[h][s][:], by_sin[h][s][:], ADD)
-            nc.sync.dma_start(out_rows[h][:, :, s * RUN : (s + 1) * RUN], keys[:])
+        def finish(adder, h, first, count, by_cos, by_sin):
+            keys = keep.tile([P, 2, count], F32, name="keys%d_%d" % (h, first))
+            adder.tensor_tensor(keys[:], by_cos[first // RUN][:, :, first % RUN : first % RUN + count], by_sin[:], ADD)
+            nc.sync.dma_start(out_rows[h][:, :, first : first + count], keys[:])
 
         nc.vector.tensor_copy(emb_s[:], scales[:].indirect(tok_list[:]))
-        nc.vector.tensor_copy(emb_w[:], words[:].indirect(tok_list[:]))
         deal_on_vector(0)
-        project(0)
+        deal_on_scalar(1)
+        quantise(0)
         for s in range(RUNS):
-            times_cos(0, s)
-        deal_on_vector(1)
-        project(1)
+            nc.vector.tensor_copy(emb_w[s][:], words[:].indirect(tok_list[:, s * RUN // 16 : (s + 1) * RUN // 16]))
+            project(0, s)
+        quantise(1)
         for s in range(RUNS):
-            times_sin(0, s)
-            finish(nc.gpsimd, 0, s)
+            project(1, s)
+        by_cos = [times_cos(0, s, "w_bf%d" % (1 - s)) for s in range(RUNS)]
         for s in range(RUNS):
-            times_cos(1, s)
-        for s in range(RUNS):
-            times_sin(1, s)
-        for s in range(RUNS):
-            finish(nc.vector, 1, s)
+            finish(nc.gpsimd, 0, s * RUN, RUN, by_cos, times_sin(0, s * RUN, RUN))
+        by_cos = [times_cos(1, s, "by_cos%d" % s) for s in range(RUNS)]
+        waiting = None
+        for first in range(0, I, LAST_RUN):
+            by_sin = times_sin(1, first, LAST_RUN)
+            if waiting is not None:
+                finish(nc.vector, 1, first - LAST_RUN, LAST_RUN, by_cos, waiting)
+            waiting = by_sin
+        finish(nc.vector, 1, I - LAST_RUN, LAST_RUN, by_cos, waiting)

@@ -40,42 +40,46 @@ def tile_attend_freshrope_kernel(tc, emb_words, emb_scales, wk, cosn, sinn, offs
         scales = keep.tile([P, T], U8, name="scales", align_bytes=64)
         cos_all = [keep.tile([P, U], F32, name="cos_all%d" % h) for h in range(HALVES)]
         sin_all = [keep.tile([P, U], F32, name="sin_all%d" % h) for h in range(HALVES)]
-        w_raw = keep.tile([P, PACK, D], F32, name="w_raw")
+        w_raw = [keep.tile([P, PACK, HALF], F32, name="w_raw%d" % h) for h in range(HALVES)]
 
         cos_rows = cosn.rearrange("(h p e) u -> h e p u", h=HALVES, e=2)
         sin_rows = sinn.rearrange("(h p e) u -> h e p u", h=HALVES, e=2)
+        w_rows = wk.rearrange("(p j) (h c) -> h p j c", j=PACK, h=HALVES)
         out_rows = out.rearrange("(h p e) i -> h p e i", h=HALVES, e=2)
 
         nc.vector.memset(scales[:].bitcast(I32), 0)
         nc.sync.dma_start(tok_list[:], offs)
-        nc.sync.dma_start(pos_list[:], offs2)
+        nc.sync.dma_start(words[:].bitcast(I32), emb_words[0].bitcast(I32))
         for r in range(4):
             nc.sync.dma_start(scales[r:P:32, :].bitcast(I32), emb_scales[0, r:16:4, :].bitcast(I32))
-        nc.sync.dma_start(w_raw[:], wk.rearrange("(p j) c -> p j c", j=PACK))
-        nc.sync.dma_start(words[:].bitcast(I32), emb_words[0].bitcast(I32))
-        for h in range(HALVES):
-            nc.sync.dma_start(cos_all[h][:], cos_rows[h, 0])
-            nc.sync.dma_start(sin_all[h][:], sin_rows[h, 0])
+        nc.sync.dma_start(w_raw[0][:], w_rows[0])
+        nc.sync.dma_start(pos_list[:], offs2)
+        nc.sync.dma_start(cos_all[0][:], cos_rows[0, 0])
+        nc.sync.dma_start(w_raw[1][:], w_rows[1])
+        nc.sync.dma_start(sin_all[0][:], sin_rows[0, 0])
+        nc.sync.dma_start(cos_all[1][:], cos_rows[1, 0])
+        nc.sync.dma_start(sin_all[1][:], sin_rows[1, 0])
 
-        emb_w = [keep.tile([P, RUN], U16, name="emb_w%d" % s, align_bytes=64) for s in range(RUNS)]
-        emb_s = keep.tile([P, I], U8, name="emb_s", align_bytes=64)
+        emb_w = keep.tile([P, I], U16, name="emb_w", align_bytes=64)
         w_bf = [keep.tile([P, 2, P * PACK], BF16, name="w_bf%d" % h, tag="w_bf%d" % h, align_bytes=64) for h in range(HALVES)]
         w_codes = [keep.tile([P, HALF], U32, name="w_codes%d" % h, align_bytes=64) for h in range(HALVES)]
         w_scales = [keep.tile([P, HALF], U8, name="w_scales%d" % h, align_bytes=64) for h in range(HALVES)]
         acc = [[psum.tile([P, 2, RUN], F32, name="acc%d%d" % (h, s)) for s in range(RUNS)] for h in range(HALVES)]
 
-        def deal_on_scalar(h):
-            for e in range(2):
-                nc.scalar.activation(
-                    w_bf[h][:, e, :].rearrange("p (m j) -> p m j", j=PACK),
-                    w_raw[:, :, h * HALF : (h + 1) * HALF].rearrange("p j (m e) -> p e m j", e=2)[:, e],
-                    COPY,
-                )
+        def deal(h, on_scalar):
+            dst = w_bf[h][:].rearrange("p e (a b j) -> p a j b e", b=2, j=PACK)
+            src = w_raw[h][:].rearrange("p j (a b e) -> p a j b e", b=2, e=2)
+            nc.scalar.copy(dst[:, :on_scalar], src[:, :on_scalar])
+            nc.vector.tensor_copy(dst[:, on_scalar:], src[:, on_scalar:])
 
-        def deal_on_vector(h):
-            nc.vector.tensor_copy(
-                w_bf[h][:].rearrange("p e (a b j) -> p a j b e", b=2, j=PACK),
-                w_raw[:, :, h * HALF : (h + 1) * HALF].rearrange("p j (a b e) -> p a j b e", b=2, e=2),
+        def deal_on_gpsimd(h):
+            nc.gpsimd.tensor_scalar(
+                w_bf[h][:].rearrange("p e (m j) -> p e m j", j=PACK),
+                w_raw[h][:].rearrange("p j (m e) -> p e m j", e=2),
+                1.0,
+                0.0,
+                MULT,
+                ADD,
             )
 
         def quantise(h):
@@ -85,7 +89,7 @@ def tile_attend_freshrope_kernel(tc, emb_words, emb_scales, wk, cosn, sinn, offs
                 in_=w_bf[h][:].rearrange("p e c -> p (e c)"),
             )
 
-        def project(h, s):
+        def project(h, s, emb_s):
             slots = slice(s * RUN, (s + 1) * RUN)
             for e in range(2):
                 cols = slice(e * P, (e + 1) * P)
@@ -93,8 +97,8 @@ def tile_attend_freshrope_kernel(tc, emb_words, emb_scales, wk, cosn, sinn, offs
                     out=acc[h][s][:, e, :],
                     lhsT=w_codes[h][:, cols].bitcast(FP8X4),
                     lhsT_scale=w_scales[h][:, cols],
-                    rhs=emb_w[s][:].bitcast(FP4X4),
-                    rhs_scale=emb_s[:, slots],
+                    rhs=emb_w[:, slots].bitcast(FP4X4),
+                    rhs_scale=emb_s[s][:],
                     start=True,
                     stop=True,
                 )
@@ -110,10 +114,10 @@ def tile_attend_freshrope_kernel(tc, emb_words, emb_scales, wk, cosn, sinn, offs
             nc.vector.tensor_tensor(product[:], acc[h][s][:], picked[:].unsqueeze(1).to_broadcast([P, 2, RUN]), MULT)
             return product
 
-        def times_sin(h, first, count):
+        def times_sin(h, first, count, tag):
             picked = look_up(sin_all[h], "sin_g%d_%d" % (h, first), first, count)
             bank = acc[h][first // RUN][:, :, first % RUN : first % RUN + count]
-            product = keep.tile([P, 2, count], F32, name="by_sin%d_%d" % (h, first))
+            product = keep.tile([P, 2, count], F32, name="by_sin", tag=tag, align_bytes=64)
             nc.vector.scalar_tensor_tensor(product[:, 0, :], bank[:, 1, :], -1.0, picked[:], MULT, MULT)
             nc.vector.tensor_tensor(product[:, 1, :], bank[:, 0, :], picked[:], MULT)
             return product
@@ -123,23 +127,26 @@ def tile_attend_freshrope_kernel(tc, emb_words, emb_scales, wk, cosn, sinn, offs
             adder.tensor_tensor(keys[:], by_cos[first // RUN][:, :, first % RUN : first % RUN + count], by_sin[:], ADD)
             nc.sync.dma_start(out_rows[h][:, :, first : first + count], keys[:])
 
-        nc.vector.tensor_copy(emb_s[:], scales[:].indirect(tok_list[:]))
-        deal_on_vector(0)
-        deal_on_scalar(1)
-        quantise(0)
-        for s in range(RUNS):
-            nc.vector.tensor_copy(emb_w[s][:], words[:].indirect(tok_list[:, s * RUN // 16 : (s + 1) * RUN // 16]))
-            project(0, s)
+        nc.vector.tensor_copy(emb_w[:], words[:].indirect(tok_list[:]))
+        emb_s = []
+        for s, tag in enumerate(("emb_s0", "w_bf0")):
+            emb_s.append(keep.tile([P, RUN], U8, name="emb_s", tag=tag, align_bytes=64))
+            nc.vector.tensor_copy(emb_s[s][:], scales[:].indirect(tok_list[:, s * RUN // 16 : (s + 1) * RUN // 16]))
+            if s == 0:
+                deal(0, 40)
+                quantise(0)
+            project(0, s, emb_s)
+        by_cos = [times_cos(0, s, "by_cos0%d" % s) for s in range(RUNS)]
+        deal_on_gpsimd(1)
         quantise(1)
         for s in range(RUNS):
-            project(1, s)
-        by_cos = [times_cos(0, s, "w_bf%d" % (1 - s)) for s in range(RUNS)]
-        for s in range(RUNS):
-            finish(nc.gpsimd, 0, s * RUN, RUN, by_cos, times_sin(0, s * RUN, RUN))
+            project(1, s, emb_s)
+        for s, tag in enumerate(("w_bf1", "by_sin01")):
+            finish(nc.gpsimd, 0, s * RUN, RUN, by_cos, times_sin(0, s * RUN, RUN, tag))
         by_cos = [times_cos(1, s, "by_cos%d" % s) for s in range(RUNS)]
         waiting = None
         for first in range(0, I, LAST_RUN):
-            by_sin = times_sin(1, first, LAST_RUN)
+            by_sin = times_sin(1, first, LAST_RUN, "by_sin1_%d" % first)
             if waiting is not None:
                 finish(nc.vector, 1, first - LAST_RUN, LAST_RUN, by_cos, waiting)
             waiting = by_sin

@@ -67,19 +67,14 @@ def tile_attend_freshrope_kernel(tc, emb_words, emb_scales, wk, cosn, sinn, offs
         acc = [[psum.tile([P, 2, RUN], F32, name="acc%d%d" % (h, s)) for s in range(RUNS)] for h in range(HALVES)]
 
         def deal(h, on_scalar):
-            dst = w_bf[h][:].rearrange("p e (a b j) -> p a j b e", b=2, j=PACK)
-            src = w_raw[h][:].rearrange("p j (a b e) -> p a j b e", b=2, e=2)
-            nc.scalar.copy(dst[:, :on_scalar], src[:, :on_scalar])
-            nc.vector.tensor_copy(dst[:, on_scalar:], src[:, on_scalar:])
-
-        def deal_on_gpsimd(h):
-            nc.gpsimd.tensor_scalar(
-                w_bf[h][:].rearrange("p e (m j) -> p e m j", j=PACK),
-                w_raw[h][:].rearrange("p j (m e) -> p e m j", e=2),
-                1.0,
-                0.0,
-                MULT,
-                ADD,
+            nc.scalar.activation(
+                w_bf[h][:].rearrange("p e (m j) -> p e m j", j=PACK)[:, :, :on_scalar],
+                w_raw[h][:].rearrange("p j (m e) -> p e m j", e=2)[:, :, :on_scalar],
+                COPY,
+            )
+            nc.vector.tensor_copy(
+                w_bf[h][:].rearrange("p e (a b j) -> p a j b e", b=2, j=PACK)[:, on_scalar // 2 :],
+                w_raw[h][:].rearrange("p j (a b e) -> p a j b e", b=2, e=2)[:, on_scalar // 2 :],
             )
 
         def quantise(h):
@@ -114,17 +109,15 @@ def tile_attend_freshrope_kernel(tc, emb_words, emb_scales, wk, cosn, sinn, offs
             nc.vector.tensor_tensor(product[:], acc[h][s][:], picked[:].unsqueeze(1).to_broadcast([P, 2, RUN]), MULT)
             return product
 
-        def times_sin(h, first, count, tag):
+        def times_sin(h, first, count, product):
             picked = look_up(sin_all[h], "sin_g%d_%d" % (h, first), first, count)
             bank = acc[h][first // RUN][:, :, first % RUN : first % RUN + count]
-            product = keep.tile([P, 2, count], F32, name="by_sin", tag=tag, align_bytes=64)
             nc.vector.scalar_tensor_tensor(product[:, 0, :], bank[:, 1, :], -1.0, picked[:], MULT, MULT)
             nc.vector.tensor_tensor(product[:, 1, :], bank[:, 0, :], picked[:], MULT)
-            return product
 
         def finish(adder, h, first, count, by_cos, by_sin):
             keys = keep.tile([P, 2, count], F32, name="keys%d_%d" % (h, first))
-            adder.tensor_tensor(keys[:], by_cos[first // RUN][:, :, first % RUN : first % RUN + count], by_sin[:], ADD)
+            adder.tensor_tensor(keys[:], by_cos[first // RUN][:, :, first % RUN : first % RUN + count], by_sin, ADD)
             nc.sync.dma_start(out_rows[h][:, :, first : first + count], keys[:])
 
         nc.vector.tensor_copy(emb_w[:], words[:].indirect(tok_list[:]))
@@ -133,21 +126,21 @@ def tile_attend_freshrope_kernel(tc, emb_words, emb_scales, wk, cosn, sinn, offs
             emb_s.append(keep.tile([P, RUN], U8, name="emb_s", tag=tag, align_bytes=64))
             nc.vector.tensor_copy(emb_s[s][:], scales[:].indirect(tok_list[:, s * RUN // 16 : (s + 1) * RUN // 16]))
             if s == 0:
-                deal(0, 40)
+                deal(0, 80)
                 quantise(0)
             project(0, s, emb_s)
         by_cos = [times_cos(0, s, "by_cos0%d" % s) for s in range(RUNS)]
-        deal_on_gpsimd(1)
+        deal(1, 80)
         quantise(1)
         for s in range(RUNS):
             project(1, s, emb_s)
         for s, tag in enumerate(("w_bf1", "by_sin01")):
-            finish(nc.gpsimd, 0, s * RUN, RUN, by_cos, times_sin(0, s * RUN, RUN, tag))
+            by_sin = keep.tile([P, 2, RUN], F32, name="by_sin0", tag=tag, align_bytes=64)
+            times_sin(0, s * RUN, RUN, by_sin[:])
+            finish(nc.gpsimd, 0, s * RUN, RUN, by_cos, by_sin[:])
         by_cos = [times_cos(1, s, "by_cos%d" % s) for s in range(RUNS)]
-        waiting = None
+        by_sin = keep.tile([P, 2, I], F32, name="by_sin1")
         for first in range(0, I, LAST_RUN):
-            by_sin = times_sin(1, first, LAST_RUN, "by_sin1_%d" % first)
-            if waiting is not None:
-                finish(nc.vector, 1, first - LAST_RUN, LAST_RUN, by_cos, waiting)
-            waiting = by_sin
-        finish(nc.vector, 1, I - LAST_RUN, LAST_RUN, by_cos, waiting)
+            times_sin(1, first, LAST_RUN, by_sin[:, :, first : first + LAST_RUN])
+        for first, count in ((0, RUN), (RUN, LAST_RUN), (RUN + LAST_RUN, LAST_RUN)):
+            finish(nc.vector, 1, first, count, by_cos, by_sin[:, :, first : first + count])

@@ -98,26 +98,27 @@ def tile_attend_freshrope_kernel(tc, emb_words, emb_scales, wk, cosn, sinn, offs
                     stop=True,
                 )
 
-        def look_up(table, name, first, count):
+        def look_up(table, name, first, count, on_vector=False):
             picked = keep.tile([P, count], F32, name=name)
-            nc.scalar.activation(picked[:], table[:].indirect(pos_list[:, first // 16 : (first + count) // 16]), COPY)
+            window = table[:].indirect(pos_list[:, first // 16 : (first + count) // 16])
+            if on_vector:
+                nc.vector.tensor_copy(picked[:], window)
+            else:
+                nc.scalar.activation(picked[:], window, COPY)
             return picked
 
-        def times_cos(h, s, tag):
+        def times_cos(h, s, product):
             picked = look_up(cos_all[h], "cos_g%d%d" % (h, s), s * RUN, RUN)
-            product = keep.tile([P, 2, RUN], F32, name="by_cos", tag=tag, align_bytes=64)
-            nc.vector.tensor_tensor(product[:], acc[h][s][:], picked[:].unsqueeze(1).to_broadcast([P, 2, RUN]), MULT)
-            return product
+            nc.vector.tensor_tensor(product, acc[h][s][:], picked[:].unsqueeze(1).to_broadcast([P, 2, RUN]), MULT)
 
-        def times_sin(h, first, count, product):
-            picked = look_up(sin_all[h], "sin_g%d_%d" % (h, first), first, count)
+        def times_sin(h, first, count, picked, product):
             bank = acc[h][first // RUN][:, :, first % RUN : first % RUN + count]
             nc.vector.scalar_tensor_tensor(product[:, 0, :], bank[:, 1, :], -1.0, picked[:], MULT, MULT)
             nc.vector.tensor_tensor(product[:, 1, :], bank[:, 0, :], picked[:], MULT)
 
         def finish(adder, h, first, count, by_cos, by_sin):
             keys = keep.tile([P, 2, count], F32, name="keys%d_%d" % (h, first))
-            adder.tensor_tensor(keys[:], by_cos[first // RUN][:, :, first % RUN : first % RUN + count], by_sin, ADD)
+            adder.tensor_tensor(keys[:], by_cos, by_sin, ADD)
             nc.sync.dma_start(out_rows[h][:, :, first : first + count], keys[:])
 
         nc.vector.tensor_copy(emb_w[:], words[:].indirect(tok_list[:]))
@@ -129,18 +130,25 @@ def tile_attend_freshrope_kernel(tc, emb_words, emb_scales, wk, cosn, sinn, offs
                 deal(0, 80)
                 quantise(0)
             project(0, s, emb_s)
-        by_cos = [times_cos(0, s, "by_cos0%d" % s) for s in range(RUNS)]
-        deal(1, 80)
+        by_cos = keep.tile([P, 2, I], F32, name="by_cos0")
+        for s in range(RUNS):
+            times_cos(0, s, by_cos[:, :, s * RUN : (s + 1) * RUN])
+        deal(1, 72)
         quantise(1)
         for s in range(RUNS):
             project(1, s, emb_s)
+        sines = [look_up(sin_all[0], "sin_g0%d" % s, s * RUN, RUN, s == 1) for s in range(RUNS)]
         for s, tag in enumerate(("w_bf1", "by_sin01")):
             by_sin = keep.tile([P, 2, RUN], F32, name="by_sin0", tag=tag, align_bytes=64)
-            times_sin(0, s * RUN, RUN, by_sin[:])
-            finish(nc.gpsimd, 0, s * RUN, RUN, by_cos, by_sin[:])
-        by_cos = [times_cos(1, s, "by_cos%d" % s) for s in range(RUNS)]
+            times_sin(0, s * RUN, RUN, sines[s], by_sin[:])
+            finish(nc.gpsimd, 0, s * RUN, RUN, by_cos[:, :, s * RUN : (s + 1) * RUN], by_sin[:])
+        by_cos = keep.tile([P, 2, I], F32, name="by_cos1")
+        for s in range(RUNS):
+            times_cos(1, s, by_cos[:, :, s * RUN : (s + 1) * RUN])
         by_sin = keep.tile([P, 2, I], F32, name="by_sin1")
         for first in range(0, I, LAST_RUN):
-            times_sin(1, first, LAST_RUN, by_sin[:, :, first : first + LAST_RUN])
-        for first, count in ((0, RUN), (RUN, LAST_RUN), (RUN + LAST_RUN, LAST_RUN)):
-            finish(nc.vector, 1, first, count, by_cos, by_sin[:, :, first : first + count])
+            picked = look_up(sin_all[1], "sin_g1_%d" % first, first, LAST_RUN)
+            times_sin(1, first, LAST_RUN, picked, by_sin[:, :, first : first + LAST_RUN])
+        for adder, first, count in ((nc.vector, 0, RUN), (nc.vector, RUN, LAST_RUN), (nc.vector, I - LAST_RUN, LAST_RUN)):
+            slots = slice(first, first + count)
+            finish(adder, 1, first, count, by_cos[:, :, slots], by_sin[:, :, slots])

@@ -40,11 +40,10 @@ def tile_attend_freshrope_kernel(tc, emb_words, emb_scales, wk, cosn, sinn, offs
         scales = keep.tile([P, T], U8, name="scales", align_bytes=64)
         cos_all = [keep.tile([P, U], F32, name="cos_all%d" % h) for h in range(HALVES)]
         sin_all = [keep.tile([P, U], F32, name="sin_all%d" % h) for h in range(HALVES)]
-        w_raw = [keep.tile([P, PACK, HALF], F32, name="w_raw%d" % h) for h in range(HALVES)]
+        w_raw = keep.tile([P, PACK, D], F32, name="w_raw")
 
         cos_rows = cosn.rearrange("(h p e) u -> h e p u", h=HALVES, e=2)
         sin_rows = sinn.rearrange("(h p e) u -> h e p u", h=HALVES, e=2)
-        w_rows = wk.rearrange("(p j) (h c) -> h p j c", j=PACK, h=HALVES)
         out_rows = out.rearrange("(h p e) i -> h p e i", h=HALVES, e=2)
 
         nc.vector.memset(scales[:].bitcast(I32), 0)
@@ -52,15 +51,14 @@ def tile_attend_freshrope_kernel(tc, emb_words, emb_scales, wk, cosn, sinn, offs
         nc.sync.dma_start(words[:].bitcast(I32), emb_words[0].bitcast(I32))
         for r in range(4):
             nc.sync.dma_start(scales[r:P:32, :].bitcast(I32), emb_scales[0, r:16:4, :].bitcast(I32))
-        nc.sync.dma_start(w_raw[0][:], w_rows[0])
+        nc.sync.dma_start(w_raw[:], wk.rearrange("(p j) c -> p j c", j=PACK))
         nc.sync.dma_start(pos_list[:], offs2)
-        nc.sync.dma_start(cos_all[0][:], cos_rows[0, 0])
-        nc.sync.dma_start(w_raw[1][:], w_rows[1])
-        nc.sync.dma_start(sin_all[0][:], sin_rows[0, 0])
-        nc.sync.dma_start(cos_all[1][:], cos_rows[1, 0])
-        nc.sync.dma_start(sin_all[1][:], sin_rows[1, 0])
+        for h in range(HALVES):
+            nc.sync.dma_start(cos_all[h][:], cos_rows[h, 0])
+            nc.sync.dma_start(sin_all[h][:], sin_rows[h, 0])
 
         emb_w = keep.tile([P, I], U16, name="emb_w", align_bytes=64)
+        emb_s = keep.tile([P, I], U8, name="emb_s", align_bytes=64)
         w_bf = [keep.tile([P, 2, P * PACK], BF16, name="w_bf%d" % h, tag="w_bf%d" % h, align_bytes=64) for h in range(HALVES)]
         w_codes = [keep.tile([P, HALF], U32, name="w_codes%d" % h, align_bytes=64) for h in range(HALVES)]
         w_scales = [keep.tile([P, HALF], U8, name="w_scales%d" % h, align_bytes=64) for h in range(HALVES)]
@@ -69,12 +67,12 @@ def tile_attend_freshrope_kernel(tc, emb_words, emb_scales, wk, cosn, sinn, offs
         def deal(h, on_scalar):
             nc.scalar.activation(
                 w_bf[h][:].rearrange("p e (m j) -> p e m j", j=PACK)[:, :, :on_scalar],
-                w_raw[h][:].rearrange("p j (m e) -> p e m j", e=2)[:, :, :on_scalar],
+                w_raw[:, :, h * HALF : (h + 1) * HALF].rearrange("p j (m e) -> p e m j", e=2)[:, :, :on_scalar],
                 COPY,
             )
             nc.vector.tensor_copy(
                 w_bf[h][:].rearrange("p e (a b j) -> p a j b e", b=2, j=PACK)[:, on_scalar // 2 :],
-                w_raw[h][:].rearrange("p j (a b e) -> p a j b e", b=2, e=2)[:, on_scalar // 2 :],
+                w_raw[:, :, h * HALF : (h + 1) * HALF].rearrange("p j (a b e) -> p a j b e", b=2, e=2)[:, on_scalar // 2 :],
             )
 
         def quantise(h):
@@ -84,7 +82,7 @@ def tile_attend_freshrope_kernel(tc, emb_words, emb_scales, wk, cosn, sinn, offs
                 in_=w_bf[h][:].rearrange("p e c -> p (e c)"),
             )
 
-        def project(h, s, emb_s):
+        def project(h, s):
             slots = slice(s * RUN, (s + 1) * RUN)
             for e in range(2):
                 cols = slice(e * P, (e + 1) * P)
@@ -93,18 +91,14 @@ def tile_attend_freshrope_kernel(tc, emb_words, emb_scales, wk, cosn, sinn, offs
                     lhsT=w_codes[h][:, cols].bitcast(FP8X4),
                     lhsT_scale=w_scales[h][:, cols],
                     rhs=emb_w[:, slots].bitcast(FP4X4),
-                    rhs_scale=emb_s[s][:],
+                    rhs_scale=emb_s[:, slots],
                     start=True,
                     stop=True,
                 )
 
-        def look_up(table, name, first, count, on_vector=False):
+        def look_up(table, name, first, count):
             picked = keep.tile([P, count], F32, name=name)
-            window = table[:].indirect(pos_list[:, first // 16 : (first + count) // 16])
-            if on_vector:
-                nc.vector.tensor_copy(picked[:], window)
-            else:
-                nc.scalar.activation(picked[:], window, COPY)
+            nc.scalar.activation(picked[:], table[:].indirect(pos_list[:, first // 16 : (first + count) // 16]), COPY)
             return picked
 
         def times_cos(h, s, product):
@@ -122,33 +116,34 @@ def tile_attend_freshrope_kernel(tc, emb_words, emb_scales, wk, cosn, sinn, offs
             nc.sync.dma_start(out_rows[h][:, :, first : first + count], keys[:])
 
         nc.vector.tensor_copy(emb_w[:], words[:].indirect(tok_list[:]))
-        emb_s = []
-        for s, tag in enumerate(("emb_s0", "w_bf0")):
-            emb_s.append(keep.tile([P, RUN], U8, name="emb_s", tag=tag, align_bytes=64))
-            nc.vector.tensor_copy(emb_s[s][:], scales[:].indirect(tok_list[:, s * RUN // 16 : (s + 1) * RUN // 16]))
-            if s == 0:
-                deal(0, 80)
-                quantise(0)
-            project(0, s, emb_s)
-        by_cos = keep.tile([P, 2, I], F32, name="by_cos0")
+        nc.vector.tensor_copy(emb_s[:], scales[:].indirect(tok_list[:]))
+        for h in range(HALVES):
+            deal(h, (44, 64)[h])
+            quantise(h)
+            for s in range(RUNS):
+                project(h, s)
+        by_cos = [keep.tile([P, 2, RUN], F32, name="by_cos0", tag="w_bf%d" % (1 - s), align_bytes=64) for s in range(RUNS)]
         for s in range(RUNS):
-            times_cos(0, s, by_cos[:, :, s * RUN : (s + 1) * RUN])
-        deal(1, 72)
-        quantise(1)
+            times_cos(0, s, by_cos[s][:])
         for s in range(RUNS):
-            project(1, s, emb_s)
-        sines = [look_up(sin_all[0], "sin_g0%d" % s, s * RUN, RUN, s == 1) for s in range(RUNS)]
-        for s, tag in enumerate(("w_bf1", "by_sin01")):
-            by_sin = keep.tile([P, 2, RUN], F32, name="by_sin0", tag=tag, align_bytes=64)
-            times_sin(0, s * RUN, RUN, sines[s], by_sin[:])
-            finish(nc.gpsimd, 0, s * RUN, RUN, by_cos[:, :, s * RUN : (s + 1) * RUN], by_sin[:])
+            by_sin = keep.tile([P, 2, RUN], F32, name="by_sin0%d" % s)
+            times_sin(0, s * RUN, RUN, look_up(sin_all[0], "sin_g0%d" % s, s * RUN, RUN), by_sin[:])
+            finish(nc.gpsimd, 0, s * RUN, RUN, by_cos[s][:], by_sin[:])
         by_cos = keep.tile([P, 2, I], F32, name="by_cos1")
         for s in range(RUNS):
             times_cos(1, s, by_cos[:, :, s * RUN : (s + 1) * RUN])
         by_sin = keep.tile([P, 2, I], F32, name="by_sin1")
         for first in range(0, I, LAST_RUN):
             picked = look_up(sin_all[1], "sin_g1_%d" % first, first, LAST_RUN)
-            times_sin(1, first, LAST_RUN, picked, by_sin[:, :, first : first + LAST_RUN])
-        for adder, first, count in ((nc.vector, 0, RUN), (nc.vector, RUN, LAST_RUN), (nc.vector, I - LAST_RUN, LAST_RUN)):
-            slots = slice(first, first + count)
-            finish(adder, 1, first, count, by_cos[:, :, slots], by_sin[:, :, slots])
+            nc.vector.tensor_tensor(
+                by_sin[:, :, first : first + LAST_RUN],
+                acc[1][first // RUN][:, :, first % RUN : first % RUN + LAST_RUN],
+                picked[:].unsqueeze(1).to_broadcast([P, 2, LAST_RUN]),
+                MULT,
+            )
+        for s in range(RUNS):
+            slots = slice(s * RUN, (s + 1) * RUN)
+            for e in range(2):
+                keys = keep.tile([P, RUN], F32, name="keys1%d%d" % (s, e))
+                nc.vector.tensor_tensor(keys[:], by_cos[:, e, slots], by_sin[:, 1 - e, slots], ADD if e else SUB)
+                nc.sync.dma_start(out_rows[1][:, e, slots], keys[:])

@@ -47,8 +47,8 @@ def tile_attend_freshrope_kernel(tc, emb_words, emb_scales, wk, cosn, sinn, offs
         out_rows = out.rearrange("(h p e) i -> h p e i", h=HALVES, e=2)
 
         nc.vector.memset(scales[:].bitcast(I32), 0)
-        nc.sync.dma_start(tok_list[:], offs)
         nc.sync.dma_start(words[:].bitcast(I32), emb_words[0].bitcast(I32))
+        nc.sync.dma_start(tok_list[:], offs)
         for r in range(4):
             nc.sync.dma_start(scales[r:P:32, :].bitcast(I32), emb_scales[0, r:16:4, :].bitcast(I32))
         nc.sync.dma_start(w_raw[:], wk.rearrange("(p j) c -> p j c", j=PACK))
@@ -96,24 +96,20 @@ def tile_attend_freshrope_kernel(tc, emb_words, emb_scales, wk, cosn, sinn, offs
                     stop=True,
                 )
 
-        def look_up(table, name, first, count):
-            picked = keep.tile([P, count], F32, name=name)
-            nc.scalar.activation(picked[:], table[:].indirect(pos_list[:, first // 16 : (first + count) // 16]), COPY)
+        def look_up(table, tag, slots):
+            picked = keep.tile([P, slots.stop - slots.start], F32, name="picked", tag=tag)
+            nc.scalar.activation(picked[:], table[:].indirect(pos_list[:, slots.start // 16 : slots.stop // 16]), COPY)
             return picked
 
-        def times_cos(h, s, product):
-            picked = look_up(cos_all[h], "cos_g%d%d" % (h, s), s * RUN, RUN)
-            nc.vector.tensor_tensor(product, acc[h][s][:], picked[:].unsqueeze(1).to_broadcast([P, 2, RUN]), MULT)
+        def multiply(product, h, slots, picked):
+            count, first = slots.stop - slots.start, slots.start % RUN
+            bank = acc[h][slots.start // RUN][:, :, first : first + count]
+            nc.vector.tensor_tensor(product, bank, picked[:].unsqueeze(1).to_broadcast([P, 2, count]), MULT)
 
-        def times_sin(h, first, count, picked, product):
-            bank = acc[h][first // RUN][:, :, first % RUN : first % RUN + count]
-            nc.vector.scalar_tensor_tensor(product[:, 0, :], bank[:, 1, :], -1.0, picked[:], MULT, MULT)
-            nc.vector.tensor_tensor(product[:, 1, :], bank[:, 0, :], picked[:], MULT)
-
-        def finish(adder, h, first, count, by_cos, by_sin):
-            keys = keep.tile([P, 2, count], F32, name="keys%d_%d" % (h, first))
-            adder.tensor_tensor(keys[:], by_cos, by_sin, ADD)
-            nc.sync.dma_start(out_rows[h][:, :, first : first + count], keys[:])
+        def finish(adder, queue, tag, h, e, slots, by_cos, by_sin):
+            keys = keep.tile([P, slots.stop - slots.start], F32, name="keys", tag=tag)
+            adder.tensor_tensor(keys[:], by_cos, by_sin, ADD if e else SUB)
+            queue.dma_start(out_rows[h][:, e, slots], keys[:])
 
         nc.vector.tensor_copy(emb_w[:], words[:].indirect(tok_list[:]))
         nc.vector.tensor_copy(emb_s[:], scales[:].indirect(tok_list[:]))
@@ -122,28 +118,32 @@ def tile_attend_freshrope_kernel(tc, emb_words, emb_scales, wk, cosn, sinn, offs
             quantise(h)
             for s in range(RUNS):
                 project(h, s)
-        by_cos = [keep.tile([P, 2, RUN], F32, name="by_cos0", tag="w_bf%d" % (1 - s), align_bytes=64) for s in range(RUNS)]
-        for s in range(RUNS):
-            times_cos(0, s, by_cos[s][:])
-        for s in range(RUNS):
-            by_sin = keep.tile([P, 2, RUN], F32, name="by_sin0%d" % s)
-            times_sin(0, s * RUN, RUN, look_up(sin_all[0], "sin_g0%d" % s, s * RUN, RUN), by_sin[:])
-            finish(nc.gpsimd, 0, s * RUN, RUN, by_cos[s][:], by_sin[:])
-        by_cos = keep.tile([P, 2, I], F32, name="by_cos1")
-        for s in range(RUNS):
-            times_cos(1, s, by_cos[:, :, s * RUN : (s + 1) * RUN])
-        by_sin = keep.tile([P, 2, I], F32, name="by_sin1")
-        for first in range(0, I, LAST_RUN):
-            picked = look_up(sin_all[1], "sin_g1_%d" % first, first, LAST_RUN)
-            nc.vector.tensor_tensor(
-                by_sin[:, :, first : first + LAST_RUN],
-                acc[1][first // RUN][:, :, first % RUN : first % RUN + LAST_RUN],
-                picked[:].unsqueeze(1).to_broadcast([P, 2, LAST_RUN]),
-                MULT,
-            )
-        for s in range(RUNS):
-            slots = slice(s * RUN, (s + 1) * RUN)
-            for e in range(2):
-                keys = keep.tile([P, RUN], F32, name="keys1%d%d" % (s, e))
-                nc.vector.tensor_tensor(keys[:], by_cos[:, e, slots], by_sin[:, 1 - e, slots], ADD if e else SUB)
-                nc.sync.dma_start(out_rows[1][:, e, slots], keys[:])
+
+        low, high = slice(0, RUN), slice(RUN, I)
+        cos0 = [keep.tile([P, 2, RUN], F32, name="cos0", tag="w_bf%d" % (1 - s), align_bytes=64) for s in range(RUNS)]
+        sin0 = [keep.tile([P, 2, RUN], F32, name="sin0%d" % s) for s in range(RUNS)]
+        cos1 = keep.tile([P, 2, I], F32, name="cos1")
+        sin1 = keep.tile([P, 2, I], F32, name="sin1")
+        for s, slots in enumerate((low, high)):
+            multiply(cos0[s][:], 0, slots, look_up(cos_all[0], "cos_g0%d" % s, slots))
+
+        picked = look_up(sin_all[0], "sin_g00", low)
+        nc.vector.scalar_tensor_tensor(sin0[0][:, 0, :], acc[0][0][:, 1, :], -1.0, picked[:], MULT, MULT)
+        nc.vector.tensor_tensor(sin0[0][:, 1, :], acc[0][0][:, 0, :], picked[:], MULT)
+        keys = keep.tile([P, 2, RUN], F32, name="keys_low")
+        nc.gpsimd.tensor_tensor(keys[:], cos0[0][:], sin0[0][:], ADD)
+        nc.sync.dma_start(out_rows[0][:, :, low], keys[:])
+        multiply(sin0[1][:], 0, high, look_up(sin_all[0], "sin_g01", high))
+        finish(nc.gpsimd, nc.sync, "keys00", 0, 0, high, cos0[1][:, 0, :], sin0[1][:, 1, :])
+
+        for s, slots in enumerate((low, high)):
+            multiply(cos1[:, :, slots], 1, slots, look_up(cos_all[1], "cos_g1%d" % s, slots))
+        quarters = [slice(first, first + LAST_RUN) for first in range(0, I, LAST_RUN)]
+        for q in range(3):
+            multiply(sin1[:, :, quarters[q]], 1, quarters[q], look_up(sin_all[1], "sin_g1%d" % q, quarters[q]))
+        finish(nc.vector, nc.sync, "sin_g11", 0, 1, high, cos0[1][:, 1, :], sin0[1][:, 0, :])
+        finish(nc.vector, nc.sync, "keys10", 1, 0, low, cos1[:, 0, low], sin1[:, 1, low])
+        multiply(sin1[:, :, quarters[3]], 1, quarters[3], look_up(sin_all[1], "sin_g13", quarters[3]))
+        for n, (e, slots) in enumerate(((1, low), (0, high), (1, quarters[2]), (1, quarters[3]))):
+            queue = nc.sync if n % 2 else nc.scalar
+            finish(nc.vector, queue, "keys1_%d" % n, 1, e, slots, cos1[:, e, slots], sin1[:, 1 - e, slots])

@@ -64,22 +64,25 @@ def tile_attend_freshrope_kernel(tc, emb_words, emb_scales, wk, cosn, sinn, offs
         w_scales = [keep.tile([P, HALF], U8, name="w_scales%d" % h, align_bytes=64) for h in range(HALVES)]
         acc = [[psum.tile([P, 2, RUN], F32, name="acc%d%d" % (h, s)) for s in range(RUNS)] for h in range(HALVES)]
 
-        def deal(h, on_scalar):
+        def deal_on_scalar(h, e, columns):
             nc.scalar.activation(
-                w_bf[h][:].rearrange("p e (m j) -> p e m j", j=PACK)[:, :, :on_scalar],
-                w_raw[:, :, h * HALF : (h + 1) * HALF].rearrange("p j (m e) -> p e m j", e=2)[:, :, :on_scalar],
+                w_bf[h][:, e, :].rearrange("p (m j) -> p m j", j=PACK)[:, columns],
+                w_raw[:, :, h * HALF : (h + 1) * HALF].rearrange("p j (m e) -> p e m j", e=2)[:, e, columns],
                 COPY,
             )
+
+        def deal_on_vector(h, e, columns):
             nc.vector.tensor_copy(
-                w_bf[h][:].rearrange("p e (a b j) -> p a j b e", b=2, j=PACK)[:, on_scalar // 2 :],
-                w_raw[:, :, h * HALF : (h + 1) * HALF].rearrange("p j (a b e) -> p a j b e", b=2, e=2)[:, on_scalar // 2 :],
+                w_bf[h][:, e, :].rearrange("p (m j) -> p m j", j=PACK)[:, columns],
+                w_raw[:, :, h * HALF : (h + 1) * HALF].rearrange("p j (m e) -> p e m j", e=2)[:, e, columns],
             )
 
-        def quantise(h):
+        def quantise(h, parities):
+            cols = slice(parities.start * P, parities.stop * P)
             nc.vector.quantize_mx(
-                out=w_codes[h][:].bitcast(FP8X4),
-                scales=w_scales[h][:],
-                in_=w_bf[h][:].rearrange("p e c -> p (e c)"),
+                out=w_codes[h][:, cols].bitcast(FP8X4),
+                scales=w_scales[h][:, cols],
+                in_=w_bf[h][:, parities, :].rearrange("p e c -> p (e c)"),
             )
 
         def project(h, s):
@@ -114,8 +117,14 @@ def tile_attend_freshrope_kernel(tc, emb_words, emb_scales, wk, cosn, sinn, offs
         nc.vector.tensor_copy(emb_w[:], words[:].indirect(tok_list[:]))
         nc.vector.tensor_copy(emb_s[:], scales[:].indirect(tok_list[:]))
         for h in range(HALVES):
-            deal(h, (44, 64)[h])
-            quantise(h)
+            deal_on_vector(h, 0, slice(0, P))
+        deal_on_scalar(0, 1, slice(0, P))
+        deal_on_scalar(1, 1, slice(0, P // 2))
+        quantise(0, slice(0, 1))
+        quantise(0, slice(1, 2))
+        deal_on_vector(1, 1, slice(P // 2, P))
+        quantise(1, slice(0, 2))
+        for h in range(HALVES):
             for s in range(RUNS):
                 project(h, s)
 

@@ -64,18 +64,16 @@ def tile_attend_freshrope_kernel(tc, emb_words, emb_scales, wk, cosn, sinn, offs
         w_scales = [keep.tile([P, HALF], U8, name="w_scales%d" % h, align_bytes=64) for h in range(HALVES)]
         acc = [[psum.tile([P, 2, RUN], F32, name="acc%d%d" % (h, s)) for s in range(RUNS)] for h in range(HALVES)]
 
-        def deal_on_scalar(h, e, columns):
-            nc.scalar.activation(
-                w_bf[h][:, e, :].rearrange("p (m j) -> p m j", j=PACK)[:, columns],
-                w_raw[:, :, h * HALF : (h + 1) * HALF].rearrange("p j (m e) -> p e m j", e=2)[:, e, columns],
-                COPY,
-            )
+        def deal_views(h, pairs):
+            dealt = w_bf[h][:].rearrange("p e (m j) -> p m j e", j=PACK)[:, pairs]
+            raw = w_raw[:, :, h * HALF : (h + 1) * HALF].rearrange("p j (m e) -> p m j e", e=2)[:, pairs]
+            return dealt, raw
 
-        def deal_on_vector(h, e, columns):
-            nc.vector.tensor_copy(
-                w_bf[h][:, e, :].rearrange("p (m j) -> p m j", j=PACK)[:, columns],
-                w_raw[:, :, h * HALF : (h + 1) * HALF].rearrange("p j (m e) -> p e m j", e=2)[:, e, columns],
-            )
+        def deal_on_scalar(h, pairs):
+            nc.scalar.activation(*deal_views(h, pairs), COPY)
+
+        def deal_on_vector(h, pairs):
+            nc.vector.tensor_copy(*deal_views(h, pairs))
 
         def quantise(h, parities):
             cols = slice(parities.start * P, parities.stop * P)
@@ -117,12 +115,12 @@ def tile_attend_freshrope_kernel(tc, emb_words, emb_scales, wk, cosn, sinn, offs
         nc.vector.tensor_copy(emb_w[:], words[:].indirect(tok_list[:]))
         nc.vector.tensor_copy(emb_s[:], scales[:].indirect(tok_list[:]))
         for h in range(HALVES):
-            deal_on_vector(h, 0, slice(0, P))
-        deal_on_scalar(0, 1, slice(0, P))
-        deal_on_scalar(1, 1, slice(0, P // 2))
+            deal_on_vector(h, slice(0, P // 2))
+        deal_on_scalar(0, slice(P // 2, P))
+        deal_on_scalar(1, slice(3 * P // 4, P))
         quantise(0, slice(0, 1))
         quantise(0, slice(1, 2))
-        deal_on_vector(1, 1, slice(P // 2, P))
+        deal_on_vector(1, slice(P // 2, 3 * P // 4))
         quantise(1, slice(0, 2))
         for h in range(HALVES):
             for s in range(RUNS):

@@ -105,7 +105,7 @@ def tile_attend_freshrope_kernel(tc, emb_words, emb_scales, wk, cosn, sinn, offs
         def multiply(product, h, slots, picked):
             count, first = slots.stop - slots.start, slots.start % RUN
             bank = acc[h][slots.start // RUN][:, :, first : first + count]
-            nc.vector.tensor_tensor(product, bank, picked[:].unsqueeze(1).to_broadcast([P, 2, count]), MULT)
+            nc.vector.tensor_tensor(product, picked[:].unsqueeze(1).to_broadcast([P, 2, count]), bank, MULT)
 
         def finish(adder, queue, tag, h, e, slots, by_cos, by_sin):
             keys = keep.tile([P, slots.stop - slots.start], F32, name="keys", tag=tag)
@@ -135,8 +135,8 @@ def tile_attend_freshrope_kernel(tc, emb_words, emb_scales, wk, cosn, sinn, offs
             multiply(cos0[s][:], 0, slots, look_up(cos_all[0], "cos_g0%d" % s, slots))
 
         picked = look_up(sin_all[0], "sin_g00", low)
-        nc.vector.scalar_tensor_tensor(sin0[0][:, 0, :], acc[0][0][:, 1, :], -1.0, picked[:], MULT, MULT)
-        nc.vector.tensor_tensor(sin0[0][:, 1, :], acc[0][0][:, 0, :], picked[:], MULT)
+        nc.vector.scalar_tensor_tensor(sin0[0][:, 0, :], picked[:], -1.0, acc[0][0][:, 1, :], MULT, MULT)
+        nc.vector.tensor_tensor(sin0[0][:, 1, :], picked[:], acc[0][0][:, 0, :], MULT)
         keys = keep.tile([P, 2, RUN], F32, name="keys_low")
         nc.gpsimd.tensor_tensor(keys[:], cos0[0][:], sin0[0][:], ADD)
         nc.sync.dma_start(out_rows[0][:, :, low], keys[:])

@@ -121,18 +121,21 @@ def tile_attend_freshrope_kernel(tc, emb_words, emb_scales, wk, cosn, sinn, offs
         quantise(0, slice(0, 1))
         quantise(0, slice(1, 2))
         deal_on_vector(1, slice(P // 2, 3 * P // 4))
+        cos_high = keep.tile([P, RUN], F32, name="cos_high", tag="w_bf0", align_bytes=64)
+        nc.vector.tensor_copy(cos_high[:, LAST_RUN:], cos_all[0][:].indirect(pos_list[:, (I - LAST_RUN) // 16 :]))
         quantise(1, slice(0, 2))
         for h in range(HALVES):
             for s in range(RUNS):
                 project(h, s)
 
         low, high = slice(0, RUN), slice(RUN, I)
-        cos0 = [keep.tile([P, 2, RUN], F32, name="cos0", tag="w_bf%d" % (1 - s), align_bytes=64) for s in range(RUNS)]
+        cos0 = [keep.tile([P, 2, RUN], F32, name="cos0%d" % s) for s in range(RUNS)]
         sin0 = [keep.tile([P, 2, RUN], F32, name="sin0%d" % s) for s in range(RUNS)]
         cos1 = keep.tile([P, 2, I], F32, name="cos1")
         sin1 = keep.tile([P, 2, I], F32, name="sin1")
-        for s, slots in enumerate((low, high)):
-            multiply(cos0[s][:], 0, slots, look_up(cos_all[0], "cos_g0%d" % s, slots))
+        multiply(cos0[0][:], 0, low, look_up(cos_all[0], "cos_g00", low))
+        nc.scalar.activation(cos_high[:, :LAST_RUN], cos_all[0][:].indirect(pos_list[:, RUN // 16 : (I - LAST_RUN) // 16]), COPY)
+        multiply(cos0[1][:], 0, high, cos_high)
 
         picked = look_up(sin_all[0], "sin_g00", low)
         nc.vector.scalar_tensor_tensor(sin0[0][:, 0, :], picked[:], -1.0, acc[0][0][:, 1, :], MULT, MULT)

@@ -135,20 +135,23 @@ def tile_attend_freshrope_kernel(tc, emb_words, emb_scales, wk, cosn, sinn, offs
         sin1 = keep.tile([P, 2, I], F32, name="sin1")
         multiply(cos0[0][:], 0, low, look_up(cos_all[0], "cos_g00", low))
         nc.scalar.activation(cos_high[:, :LAST_RUN], cos_all[0][:].indirect(pos_list[:, RUN // 16 : (I - LAST_RUN) // 16]), COPY)
-        multiply(cos0[1][:], 0, high, cos_high)
 
-        picked = look_up(sin_all[0], "sin_g00", low)
-        nc.vector.scalar_tensor_tensor(sin0[0][:, 0, :], picked[:], -1.0, acc[0][0][:, 1, :], MULT, MULT)
-        nc.vector.tensor_tensor(sin0[0][:, 1, :], picked[:], acc[0][0][:, 0, :], MULT)
-        keys = keep.tile([P, 2, RUN], F32, name="keys_low")
-        nc.gpsimd.tensor_tensor(keys[:], cos0[0][:], sin0[0][:], ADD)
-        nc.sync.dma_start(out_rows[0][:, :, low], keys[:])
-        multiply(sin0[1][:], 0, high, look_up(sin_all[0], "sin_g01", high))
+        quarters = [slice(first, first + LAST_RUN) for first in range(0, I, LAST_RUN)]
+
+        for q in range(2):
+            picked = look_up(sin_all[0], "sin_g0%d" % q, quarters[q])
+            nc.vector.scalar_tensor_tensor(sin0[0][:, 0, quarters[q]], picked[:], -1.0, acc[0][0][:, 1, quarters[q]], MULT, MULT)
+            nc.vector.tensor_tensor(sin0[0][:, 1, quarters[q]], picked[:], acc[0][0][:, 0, quarters[q]], MULT)
+            keys = keep.tile([P, 2, LAST_RUN], F32, name="keys_low%d" % q)
+            nc.gpsimd.tensor_tensor(keys[:], cos0[0][:, :, quarters[q]], sin0[0][:, :, quarters[q]], ADD)
+            nc.sync.dma_start(out_rows[0][:, :, quarters[q]], keys[:])
+            if q == 0:
+                multiply(cos0[1][:], 0, high, cos_high)
+        multiply(sin0[1][:], 0, high, look_up(sin_all[0], "sin_g02", high))
         finish(nc.gpsimd, nc.sync, "keys00", 0, 0, high, cos0[1][:, 0, :], sin0[1][:, 1, :])
 
-        for s, slots in enumerate((low, high)):
-            multiply(cos1[:, :, slots], 1, slots, look_up(cos_all[1], "cos_g1%d" % s, slots))
-        quarters = [slice(first, first + LAST_RUN) for first in range(0, I, LAST_RUN)]
+        for n, slots in enumerate((low, quarters[2], quarters[3])):
+            multiply(cos1[:, :, slots], 1, slots, look_up(cos_all[1], "cos_g1%d" % n, slots))
         for q in range(3):
             multiply(sin1[:, :, quarters[q]], 1, quarters[q], look_up(sin_all[1], "sin_g1%d" % q, quarters[q]))
         finish(nc.vector, nc.sync, "sin_g11", 0, 1, high, cos0[1][:, 1, :], sin0[1][:, 0, :])

@@ -145,16 +145,16 @@ def tile_attend_freshrope_kernel(tc, emb_words, emb_scales, wk, cosn, sinn, offs
             keys = keep.tile([P, 2, LAST_RUN], F32, name="keys_low%d" % q)
             nc.gpsimd.tensor_tensor(keys[:], cos0[0][:, :, quarters[q]], sin0[0][:, :, quarters[q]], ADD)
             nc.sync.dma_start(out_rows[0][:, :, quarters[q]], keys[:])
-            if q == 0:
-                multiply(cos0[1][:], 0, high, cos_high)
+        multiply(cos0[1][:], 0, high, cos_high)
         multiply(sin0[1][:], 0, high, look_up(sin_all[0], "sin_g02", high))
         finish(nc.gpsimd, nc.sync, "keys00", 0, 0, high, cos0[1][:, 0, :], sin0[1][:, 1, :])
+        finish(nc.gpsimd, nc.sync, "keys01", 0, 1, quarters[2], cos0[1][:, 1, quarters[0]], sin0[1][:, 0, quarters[0]])
 
         for n, slots in enumerate((low, quarters[2], quarters[3])):
             multiply(cos1[:, :, slots], 1, slots, look_up(cos_all[1], "cos_g1%d" % n, slots))
         for q in range(3):
             multiply(sin1[:, :, quarters[q]], 1, quarters[q], look_up(sin_all[1], "sin_g1%d" % q, quarters[q]))
-        finish(nc.vector, nc.sync, "sin_g11", 0, 1, high, cos0[1][:, 1, :], sin0[1][:, 0, :])
+        finish(nc.vector, nc.sync, "sin_g11", 0, 1, quarters[3], cos0[1][:, 1, quarters[1]], sin0[1][:, 0, quarters[1]])
         finish(nc.vector, nc.sync, "keys10", 1, 0, low, cos1[:, 0, low], sin1[:, 1, low])
         multiply(sin1[:, :, quarters[3]], 1, quarters[3], look_up(sin_all[1], "sin_g13", quarters[3]))
         for n, (e, slots) in enumerate(((1, low), (0, high), (1, quarters[2]), (1, quarters[3]))):

@@ -155,8 +155,9 @@ def tile_attend_freshrope_kernel(tc, emb_words, emb_scales, wk, cosn, sinn, offs
         for q in range(3):
             multiply(sin1[:, :, quarters[q]], 1, quarters[q], look_up(sin_all[1], "sin_g1%d" % q, quarters[q]))
         finish(nc.vector, nc.sync, "sin_g11", 0, 1, quarters[3], cos0[1][:, 1, quarters[1]], sin0[1][:, 0, quarters[1]])
-        finish(nc.vector, nc.sync, "keys10", 1, 0, low, cos1[:, 0, low], sin1[:, 1, low])
+        for e in range(2):
+            finish(nc.vector, nc.sync, "keys1%d" % e, 1, e, low, cos1[:, e, low], sin1[:, 1 - e, low])
         multiply(sin1[:, :, quarters[3]], 1, quarters[3], look_up(sin_all[1], "sin_g13", quarters[3]))
-        for n, (e, slots) in enumerate(((1, low), (0, high), (1, quarters[2]), (1, quarters[3]))):
-            queue = nc.sync if n % 2 else nc.scalar
-            finish(nc.vector, queue, "keys1_%d" % n, 1, e, slots, cos1[:, e, slots], sin1[:, 1 - e, slots])
+        for slots in quarters[2:]:
+            for e, queue in enumerate((nc.scalar, nc.sync)):
+                finish(nc.vector, queue, "keys1%d_%d" % (e, slots.start), 1, e, slots, cos1[:, e, slots], sin1[:, 1 - e, slots])

@@ -117,10 +117,9 @@ def tile_attend_freshrope_kernel(tc, emb_words, emb_scales, wk, cosn, sinn, offs
         for h in range(HALVES):
             deal_on_vector(h, slice(0, P // 2))
         deal_on_scalar(0, slice(P // 2, P))
-        deal_on_scalar(1, slice(3 * P // 4, P))
+        deal_on_scalar(1, slice(P // 2, P))
         quantise(0, slice(0, 1))
         quantise(0, slice(1, 2))
-        deal_on_vector(1, slice(P // 2, 3 * P // 4))
         cos_high = keep.tile([P, RUN], F32, name="cos_high", tag="w_bf0", align_bytes=64)
         nc.vector.tensor_copy(cos_high[:, LAST_RUN:], cos_all[0][:].indirect(pos_list[:, (I - LAST_RUN) // 16 :]))
         quantise(1, slice(0, 2))

from contextlib import ExitStack

import concourse.mybir as mybir

K, T, I, D, U = 512, 2048, 512, 512, 1024
FLOPS = 2 * K * D * I
BYTES = 128 * 4096 + 16 * 2048 + K * D * 4 + 2 * (D // 2) * U * 4 + 2 * 128 * 32 * 2 + D * I * 4

F32 = mybir.dt.float32
BF16 = mybir.dt.bfloat16
I32 = mybir.dt.int32
U32 = mybir.dt.uint32
U16 = mybir.dt.uint16
U8 = mybir.dt.uint8
FP8X4 = mybir.dt.float8_e4m3fn_x4
FP4X4 = mybir.dt.float4_e2m1fn_x4
MULT = mybir.AluOpType.mult
ADD = mybir.AluOpType.add
SUB = mybir.AluOpType.subtract
COPY = mybir.ActivationFunctionType.Copy

P = 128
PACK = 4
HALVES = 2
HALF = D // HALVES
RUNS = 2
RUN = I // RUNS
LAST_RUN = RUN // 2


def tile_attend_freshrope_kernel(tc, emb_words, emb_scales, wk, cosn, sinn, offs, offs2, out):
    nc = tc.nc
    with ExitStack() as ctx:
        keep = ctx.enter_context(tc.tile_pool(name="keep", bufs=1))
        psum = ctx.enter_context(tc.psum_pool(name="psum", bufs=1))

        tok_list = keep.tile([P, I // 16], U16, name="tok_list")
        pos_list = keep.tile([P, I // 16], U16, name="pos_list")
        words = keep.tile([P, T], U16, name="words", align_bytes=64)
        scales = keep.tile([P, T], U8, name="scales", align_bytes=64)
        cos_all = [keep.tile([P, U], F32, name="cos_all%d" % h) for h in range(HALVES)]
        sin_all = [keep.tile([P, U], F32, name="sin_all%d" % h) for h in range(HALVES)]
        w_raw = keep.tile([P, PACK, D], F32, name="w_raw")

        cos_rows = cosn.rearrange("(h p e) u -> h e p u", h=HALVES, e=2)
        sin_rows = sinn.rearrange("(h p e) u -> h e p u", h=HALVES, e=2)
        out_rows = out.rearrange("(h p e) i -> h p e i", h=HALVES, e=2)

        nc.vector.memset(scales[:].bitcast(I32), 0)
        nc.sync.dma_start(words[:].bitcast(I32), emb_words[0].bitcast(I32))
        nc.sync.dma_start(tok_list[:], offs)
        for r in range(4):
            nc.sync.dma_start(scales[r:P:32, :].bitcast(I32), emb_scales[0, r:16:4, :].bitcast(I32))
        nc.sync.dma_start(w_raw[:], wk.rearrange("(p j) c -> p j c", j=PACK))
        nc.sync.dma_start(pos_list[:], offs2)
        for h in range(HALVES):
            nc.sync.dma_start(cos_all[h][:], cos_rows[h, 0])
            nc.sync.dma_start(sin_all[h][:], sin_rows[h, 0])

        emb_w = keep.tile([P, I], U16, name="emb_w", align_bytes=64)
        emb_s = keep.tile([P, I], U8, name="emb_s", align_bytes=64)
        w_bf = [keep.tile([P, 2, P * PACK], BF16, name="w_bf%d" % h, tag="w_bf%d" % h, align_bytes=64) for h in range(HALVES)]
        w_codes = [keep.tile([P, HALF], U32, name="w_codes%d" % h, align_bytes=64) for h in range(HALVES)]
        w_scales = [keep.tile([P, HALF], U8, name="w_scales%d" % h, align_bytes=64) for h in range(HALVES)]
        acc = [[psum.tile([P, 2, RUN], F32, name="acc%d%d" % (h, s)) for s in range(RUNS)] for h in range(HALVES)]

        def deal_views(h, pairs):
            dealt = w_bf[h][:].rearrange("p e (m j) -> p m j e", j=PACK)[:, pairs]
            raw = w_raw[:, :, h * HALF : (h + 1) * HALF].rearrange("p j (m e) -> p m j e", e=2)[:, pairs]
            return dealt, raw

        def deal_on_scalar(h, pairs):
            nc.scalar.activation(*deal_views(h, pairs), COPY)

        def deal_on_vector(h, pairs):
            nc.vector.tensor_copy(*deal_views(h, pairs))

        def quantise(h, parities):
            cols = slice(parities.start * P, parities.stop * P)
            nc.vector.quantize_mx(
                out=w_codes[h][:, cols].bitcast(FP8X4),
                scales=w_scales[h][:, cols],
                in_=w_bf[h][:, parities, :].rearrange("p e c -> p (e c)"),
            )

        def project(h, s):
            slots = slice(s * RUN, (s + 1) * RUN)
            for e in range(2):
                cols = slice(e * P, (e + 1) * P)
                nc.tensor.matmul_mx(
                    out=acc[h][s][:, e, :],
                    lhsT=w_codes[h][:, cols].bitcast(FP8X4),
                    lhsT_scale=w_scales[h][:, cols],
                    rhs=emb_w[:, slots].bitcast(FP4X4),
                    rhs_scale=emb_s[:, slots],
                    start=True,
                    stop=True,
                )

        def look_up(table, tag, slots):
            picked = keep.tile([P, slots.stop - slots.start], F32, name="picked", tag=tag)
            nc.scalar.activation(picked[:], table[:].indirect(pos_list[:, slots.start // 16 : slots.stop // 16]), COPY)
            return picked

        def multiply(product, h, slots, picked):
            count, first = slots.stop - slots.start, slots.start % RUN
            bank = acc[h][slots.start // RUN][:, :, first : first + count]
            nc.vector.tensor_tensor(product, picked[:].unsqueeze(1).to_broadcast([P, 2, count]), bank, MULT)

        def finish(adder, queue, tag, h, e, slots, by_cos, by_sin):
            keys = keep.tile([P, slots.stop - slots.start], F32, name="keys", tag=tag)
            adder.tensor_tensor(keys[:], by_cos, by_sin, ADD if e else SUB)
            queue.dma_start(out_rows[h][:, e, slots], keys[:])

        nc.vector.tensor_copy(emb_w[:], words[:].indirect(tok_list[:]))
        nc.vector.tensor_copy(emb_s[:], scales[:].indirect(tok_list[:]))
        for h in range(HALVES):
            deal_on_vector(h, slice(0, P // 2))
        deal_on_scalar(0, slice(P // 2, P))
        deal_on_scalar(1, slice(P // 2, P))
        quantise(0, slice(0, 1))
        quantise(0, slice(1, 2))
        cos_high = keep.tile([P, RUN], F32, name="cos_high", tag="w_bf0", align_bytes=64)
        nc.vector.tensor_copy(cos_high[:, LAST_RUN:], cos_all[0][:].indirect(pos_list[:, (I - LAST_RUN) // 16 :]))
        quantise(1, slice(0, 2))
        for h in range(HALVES):
            for s in range(RUNS):
                project(h, s)

        low, high = slice(0, RUN), slice(RUN, I)
        cos0 = [keep.tile([P, 2, RUN], F32, name="cos0%d" % s) for s in range(RUNS)]
        sin0 = [keep.tile([P, 2, RUN], F32, name="sin0%d" % s) for s in range(RUNS)]
        cos1 = keep.tile([P, 2, I], F32, name="cos1")
        sin1 = keep.tile([P, 2, I], F32, name="sin1")
        multiply(cos0[0][:], 0, low, look_up(cos_all[0], "cos_g00", low))
        nc.scalar.activation(cos_high[:, :LAST_RUN], cos_all[0][:].indirect(pos_list[:, RUN // 16 : (I - LAST_RUN) // 16]), COPY)

        quarters = [slice(first, first + LAST_RUN) for first in range(0, I, LAST_RUN)]

        for q in range(2):
            picked = look_up(sin_all[0], "sin_g0%d" % q, quarters[q])
            nc.vector.scalar_tensor_tensor(sin0[0][:, 0, quarters[q]], picked[:], -1.0, acc[0][0][:, 1, quarters[q]], MULT, MULT)
            nc.vector.tensor_tensor(sin0[0][:, 1, quarters[q]], picked[:], acc[0][0][:, 0, quarters[q]], MULT)
            keys = keep.tile([P, 2, LAST_RUN], F32, name="keys_low%d" % q)
            nc.gpsimd.tensor_tensor(keys[:], cos0[0][:, :, quarters[q]], sin0[0][:, :, quarters[q]], ADD)
            nc.sync.dma_start(out_rows[0][:, :, quarters[q]], keys[:])
        multiply(cos0[1][:], 0, high, cos_high)
        multiply(sin0[1][:], 0, high, look_up(sin_all[0], "sin_g02", high))
        finish(nc.gpsimd, nc.sync, "keys00", 0, 0, high, cos0[1][:, 0, :], sin0[1][:, 1, :])
        finish(nc.gpsimd, nc.sync, "keys01", 0, 1, quarters[2], cos0[1][:, 1, quarters[0]], sin0[1][:, 0, quarters[0]])

        for n, slots in enumerate((low, quarters[2], quarters[3])):
            multiply(cos1[:, :, slots], 1, slots, look_up(cos_all[1], "cos_g1%d" % n, slots))
        for q in range(3):
            multiply(sin1[:, :, quarters[q]], 1, quarters[q], look_up(sin_all[1], "sin_g1%d" % q, quarters[q]))
        finish(nc.vector, nc.sync, "sin_g11", 0, 1, quarters[3], cos0[1][:, 1, quarters[1]], sin0[1][:, 0, quarters[1]])
        for e in range(2):
            finish(nc.vector, nc.sync, "keys1%d" % e, 1, e, low, cos1[:, e, low], sin1[:, 1 - e, low])
        multiply(sin1[:, :, quarters[3]], 1, quarters[3], look_up(sin_all[1], "sin_g13", quarters[3]))
        for slots in quarters[2:]:
            for e, queue in enumerate((nc.scalar, nc.sync)):
                finish(nc.vector, queue, "keys1%d_%d" % (e, slots.start), 1, e, slots, cos1[:, e, slots], sin1[:, 1 - e, slots])
